import numpy as np, ml_dtypes
CORES = [35,38,43,46]
N = 4
import mx_ref
BF = ml_dtypes.bfloat16
def entries(a):
    return np.ascontiguousarray(a.T).reshape(-1)
def table(e):
    return np.ascontiguousarray(np.reshape(e, (-1, 16)).T).astype(np.int32)
def pick(q, e):
    c = np.concatenate([q[0].reshape(128, -1, 4), np.zeros((128, 1, 4), np.uint8)], axis=1); s = np.concatenate([q[1], np.ones((16, 1), np.uint8)], axis=1)
    return (np.ascontiguousarray(c[:, e].reshape(128, -1)), np.ascontiguousarray(s[:, e]))
def join(*qs):
    return (np.concatenate([q[0] for q in qs], axis=1), np.concatenate([q[1] for q in qs], axis=1))
def put(q, e, v):
    c, s = q[0].reshape(128, -1, 4).copy(), q[1].copy(); c[:, e] = v[0].reshape(128, -1, 4); s[:, e] = v[1]
    return (c.reshape(128, -1), s)
def pk(c, s):
    return (np.ascontiguousarray(c), mx_ref.live(s))
def emit(q):
    return q[0], q[1]
def packed(v, rng):
    q = [mx_ref.quantize(np.ascontiguousarray(v[r])) for r in range(N)]
    return np.stack([a for a, b in q]), np.stack([mx_ref.plane(b, rng) for a, b in q])
def f(rng, *shape):
    return mx_ref.flush((rng.standard_normal(shape, dtype=np.float32) * np.exp2(rng.integers(-2, 3, shape[:-1] + (1,)))).astype(BF))
def wide(rng, *shape, cols=0):
    v = rng.standard_normal(shape, dtype=np.float32) * np.exp2(rng.integers(-12, 13, shape)).astype(np.float32)
    if cols: v *= np.repeat(np.exp2(rng.integers(-cols, cols + 1, shape[:-2] + (1, shape[-1] // 4))) * (rng.random(shape[:-2] + (1, shape[-1] // 4)) > 0.0625), 4, axis=-1).astype(np.float32)
    return mx_ref.flush(v.astype(BF))
C, CB, CAPP, S = 512, 288, 176, 640
def counts(rng, total, cap, least):
    n = np.array(least)
    while n.sum() < total: n[rng.choice(np.flatnonzero(n < cap))] += 1
    return n
def runs(rng, least, cap):
    n = np.zeros((N, N), int)
    for s in range(N)[::-1]: n[s] = counts(rng, C, np.minimum(cap[s], CAPP + n[N - 1]), least[s])
    return n
def keeps(rng, n, fall=0, least=np.zeros((N, N), int)):
    k = np.zeros((N, N), int)
    for s in range(N)[::-1]:
        above = k.sum(axis=0)
        k[s] = np.clip(np.minimum(rng.integers(0, 2 * n[s] // 3 + 1), n[s] - fall), np.maximum(n[s] - above, least[s]), np.minimum(np.minimum(n[s], CAPP), S - above))
    return k
def lists(rng, n, k, ends=False, narrow=False):
    p = np.sort(rng.choice(65536 - 2 * N * S, N - 1, replace=False)) + 2 * S * np.arange(1, N)
    if ends: p[0] = int(k[:, 0].sum()) + 2 + int(rng.integers(0, 4))
    if narrow: p[-1] = 65535
    lo, hi = np.append(0, p), np.append(p, 65536)
    keys = [[] for s in range(N)]
    for d in range(N):
        e, i, j = int(ends), -1, -1
        u = lo[d] + e + rng.choice(int(hi[d] - lo[d]) - 2 * e, int(k[:, d].sum()), replace=False)
        at = np.append(np.cumsum(k[::-1, d])[::-1], 0)[1:]
        if ends:
            low, c = np.flatnonzero(n[:, d] - k[:, d] > 1), np.flatnonzero(k[:, d] > 1)
            c = c[c > low[0]]
            if d in (0, N - 1): c = c[c < N - 1]
            i = rng.choice(c); j = rng.choice(low[low < i])
            u[at[i]] = lo[d]; u[at[i] + 1] = hi[d] - 1
        for s in range(N):
            m = at[i] + np.arange(2) if s == j else np.zeros(0, int)
            old = np.concatenate([m, rng.permutation(np.setdiff1d(np.arange(at[s]), m))])[:n[s, d] - k[s, d]]
            keys[s].append(u[np.concatenate([old, at[s] + np.arange(k[s, d])])])
    return {"ky": np.stack([table(np.sort(np.concatenate(v))) for v in keys]), "sp": np.stack([table(np.append(p, np.full(17 - N, 65535)))] * N)}
def setup_inputs(rng):
    kc, ks = packed(f(rng, N, 128, 4 * C), rng)
    n = runs(rng, rng.integers(1, CAPP // 2 + 1, (N, N)), np.full((N, N), CB))
    return {"kc": kc, "ks": ks, "w": f(rng, N, 128, 512), **lists(rng, n, keeps(rng, n))}
def setup_inputs_single(rng):
    least, cap = rng.integers(1, CAPP // 2 + 1, (N, N)), np.full((N, N), CB)
    least[:, N - 1] = rng.integers(0, 2, N); least[rng.permutation(N - 1)[:2], N - 1] = 1; cap[:, N - 1] = least[:, N - 1]
    n = runs(rng, least, cap)
    return {**setup_inputs(rng), **lists(rng, n, keeps(rng, n), narrow=True)}
def setup_inputs_narrow(rng):
    least, cap = rng.integers(1, CAPP // 2 + 1, (N, N)), np.full((N, N), CB)
    least[:, N - 1] = 0; cap[:, N - 1] = 0
    n = runs(rng, least, cap)
    return {**setup_inputs(rng), **lists(rng, n, keeps(rng, n), narrow=True)}
def setup_inputs_full(rng):
    h = int(rng.integers(0, N)); least = np.ones((N, N), int)
    a = np.append(h, rng.permutation(np.delete(np.arange(N), h)))[:(C - N) // CAPP]
    least[N - 1, a] = CAPP
    for s in range(N - 1): least[s, np.append(h, rng.permutation(a[1:]))[:(C - N) // CB]] = CB
    n = runs(rng, least, np.full((N, N), CB)); k = keeps(rng, n)
    v = np.zeros(N, int); v[N - 2:] = CAPP; v[rng.permutation(N - 2)[:S // CAPP - 2]] = CAPP
    k[:, h] = counts(rng, S, CAPP, v)
    return {**setup_inputs(rng), **lists(rng, n, k)}
def setup_inputs_edges(rng):
    q = int(rng.integers(1, N)); h = int(rng.choice(np.delete(np.arange(N - 1), min(q, N - 2))))
    least, cap = rng.integers(2, CAPP // 2 + 1, (N, N)), np.full((N, N), CB)
    least[h, q] = 0; cap[h, q] = 0
    few = rng.integers(2, 5, N)
    few[rng.permutation(np.setdiff1d(np.arange(N), [int(rng.integers(0, N - 2)), N - 2]))[:int(rng.integers(2, N - 1))]] = 0
    least[:, 0] = few; cap[:, 0] = few
    n = runs(rng, least, cap)
    two = np.zeros((N, N), int); two[N - 2, [0, N - 1]] = 2
    return {**setup_inputs(rng), **lists(rng, n, keeps(rng, n, 2, two), ends=True)}
def setup_inputs_spread(rng):
    d = setup_inputs(rng); d["kc"], d["ks"] = packed(wide(rng, N, 128, 4 * C, cols=8), rng); return d
def check_inputs(d):
    b = []
    p = entries(d["sp"][0]).astype(np.int64); g = p[:N - 1]
    if (d["sp"] != d["sp"][:1]).any() or (p[N - 1:] != 65535).any() or g.min() < 1 or g.max() > 65535 or (np.diff(g) <= 0).any(): b.append("sp")
    lo, hi = np.append(0, g), np.append(g, 65536)
    k = [entries(d["ky"][s]).astype(np.int64) for s in range(N)]
    bad = any(v.min() < 0 or v.max() > 65535 or (np.diff(v) <= 0).any() for v in k)
    x, s = np.concatenate(k), np.repeat(np.arange(N), C)
    o = np.argsort(x, kind="stable"); o = o[np.append(x[o][1:] != x[o][:-1], True)]
    x, s = x[o], s[o]
    for q in range(N):
        m = (x >= lo[q]) & (x < hi[q])
        if max(((v >= lo[q]) & (v < hi[q])).sum() for v in k) > CB or m.sum() > S or np.bincount(s[m], minlength=N).max() > CAPP: bad = True
    if bad: b.append("ky")
    return b
def reference(kc, ks, w, ky, sp):
    every = join(*[pk(kc[s], ks[s]) for s in range(N)])
    keys = np.concatenate([entries(ky[s]) for s in range(N)])
    oc, osc = np.zeros((N, 128, 4 * S), np.uint8), np.zeros((N, 16, S), np.uint8)
    ok, y = np.zeros((N, 2, S), np.float32), np.zeros((N, 128, S), np.float32)
    for d in range(N):
        p = entries(sp[d])[:N - 1]
        lo, hi = np.append(0, p)[d], np.append(p, 65536)[d]
        e = np.flatnonzero((keys >= lo) & (keys < hi))
        e = e[np.argsort(keys[e], kind="stable")]
        e = e[np.append(keys[e][1:] != keys[e][:-1], True)[:e.size]]
        a = np.full(S, -1); a[:e.size] = e
        kept = pick(every, a)
        oc[d], osc[d] = emit(kept)
        ok[d, 0] = np.where(a >= 0, keys[a], -1); ok[d, 1] = np.where(a >= 0, a // C, -1)
        y[d] = mx_ref.matmul(mx_ref.quantize(np.ascontiguousarray(w[d])), kept)
    return {"oc": oc, "osc": osc, "ok": ok, "y": y}

@@ -1,0 +1,312 @@
+from concourse.bass import DstId, RemoteDMATransfer
+from concourse.mybir import dt, AluOpType as OP, AxisListType, ActivationFunctionType as AF
+
+N, C, S, CAPP = 4, 512, 640, 176
+SL = 192
+NB = SL // 32
+NS = N * SL
+Z0 = 32
+BIG = 70000.0
+CH = 320
+
+
+def _s(n, d="float32"):
+    return ("sbuf", [128, n], d)
+
+
+X4, U8, U16, BF, I32 = "float8_e4m3fn_x4", "uint8", "uint16", "bfloat16", "int32"
+SCRATCH = {
+    "kl": _s(4, I32), "lki": _s(32, I32), "spi": _s(1, I32), "wt": _s(512, BF), "kcs": _s(C, X4), "kss": _s(C, U8),
+    "pidx": _s(1, I32), "pm": _s(4, I32), "pf": _s(4), "ones": _s(32), "i_exp": _s(32, I32), "expk": _s(32, U16),
+    "i_sel": _s(16), "sel": _s(16, U16), "i_e3": _s(12), "exp3": _s(12, U16), "i_d2": _s(16), "d2": _s(16), "i_d3": _s(24), "d3": _s(24),
+    "i_vj": _s(256), "vj": _s(256), "i_v3": _s(384), "v3": _s(384), "zt": _s(512, BF), "zc": _s(128, X4), "zs": _s(128, U8), "d2p": _s(16),
+    "lkf": _s(32), "at": _s(32), "spf": _s(1), "spx": _s(32), "spb": _s(32), "r1": _s(16), "r2": _s(16), "r3": _s(16), "r12": _s(16), "rr": _s(16),
+    "xa": _s(512), "fa": _s(512), "fs": _s(256), "vk": _s(256),
+    "kb": _s(12, I32), "x1": _s(384), "b1": _s(384), "b1u": _s(384, U16), "cmp": _s(16 * 384, BF), "sc": _s(16 * 192, BF), "js": _s(8 * 384, BF),
+    "rc": _s(16), "qu": _s(16), "qv": _s(16), "qo": _s(16), "fl": _s(16),
+    "q0": _s(16), "tot": _s(1), "ct": _s(64), "ctt": _s(64), "st": _s(64), "bt": _s(32), "qq": _s(16), "e1": _s(16), "e2": _s(16), "o1": _s(16), "o2": _s(16), "off": _s(16, U16),
+    "wk": _s(NS + 256), "wj": _s(NS + 256), "tk": _s(NS), "tj": _s(NS), "zk": _s(24), "kz": _s(24), "zj": _s(32),
+    "sw1": _s(32), "sw2": _s(64), "sw3": _s(64), "lj": _s(48, U16),
+    "pc0": _s(CAPP, X4), "pc1": _s(CAPP, X4), "pc2": _s(CAPP, X4), "pc3": _s(CAPP, X4),
+    "ps0": _s(CAPP, U8), "ps1": _s(CAPP, U8), "ps2": _s(CAPP, U8), "ps3": _s(CAPP, U8),
+    "ap": _s(24), "x3": _s(SL), "b3": _s(SL), "b3u": _s(SL, U16), "cmp3": _s(24 * SL, BF), "sc3": _s(24 * SL // 2, BF), "j3": _s(24 * SL, BF), "rs3": _s(24),
+    "rc3": _s(24), "qu3": _s(24), "qv3": _s(24), "qo3": _s(24), "vm": _s(24), "vd1": _s(24), "vd": _s(24), "p1": _s(24), "p2": _s(24), "off3": _s(24, U16),
+    "wo": _s(S + 384), "to": _s(S), "zo": _s(32), "so1": _s(32), "so2": _s(64), "so3": _s(64), "lf": _s(40, U16),
+    "fw": _s(Z0 + NS, X4), "fsc": _s(Z0 + NS, U8), "oq": _s(S, X4), "os_": _s(S, U8), "wq": _s(128, X4), "wsc": _s(128, U8),
+    "kf": _s(Z0 + NS), "okf": _s(S), "yw": _s(Z0 + NS), "ys": _s(S), "pz": ("psum", [128, 512 * N], "float32"),
+}
+SEMAPHORES = ["v", "s", "t", "gi", "dkl", "dlk", "dsp", "dw", "dk", "dz", "kin", "slk", "colc", "cols", "lsent", "own", "st1", "st2"]
+
+
+def rank_program(g, core, T, topo):
+    r = T.rank_of(core)
+    if r is None:
+        return
+    Q = {"v": g.vector, "s": g.scalar, "t": g.tensor, "g": g, "y": g.sync}
+    seen, total = {}, {}
+
+    def need(q, toks):
+        for tok in toks:
+            if tok is not None and seen.get((q, tok[0]), 0) < tok[1]:
+                Q[q].wait_ge(T.sem[tok[0]], tok[1])
+                seen[(q, tok[0])] = tok[1]
+
+    def done(inst, sem, n=1):
+        inst.then_inc(T.sem[sem], n)
+        total[sem] = total.get(sem, 0) + n
+        return (sem, total[sem])
+
+    vec, act = g.vector, g.scalar
+
+    def vop(deps, name, *a):
+        need("v", deps)
+        f = {"copy": vec.tensor_copy, "tt": vec.tensor_tensor, "ts": vec.tensor_scalar, "tr": vec.transpose, "scan": vec.tensor_tensor_scan,
+             "red": vec.tensor_reduce, "set": vec.memset, "q": vec.quantize_mx}[name]
+        return done(f(*a), "v")
+
+    def sop(deps, *a, **k):
+        need("s", deps)
+        return done(act.activation(*a, **k), "s")
+
+    def dma(q, deps, out, in_, sem):
+        need(q, deps)
+        return done(Q[q].dma_start(out, in_), sem, 16)
+
+    others = [d for d in range(N) if d != r]
+    far = [d for d in others if topo.chip(T.cores[d]) != topo.chip(core)]
+    near = [d for d in others if d not in far]
+    fe = topo.engines(core, T.cores[far[0]])
+    k = len(fe) // len(far)
+    eng = {d: fe[i * k:(i + 1) * k] for i, d in enumerate(far)}
+    for d in near:
+        eng[d] = [e for e in topo.engines(core, T.cores[d]) if e not in fe]
+    KE = k
+
+    def send(dests, sem, src, dst, few):
+        tr = []
+        for d in dests:
+            rid, pid, _ = topo.addr(T.cores[d])
+            m = sum(1 << e for e in (eng[d][:KE] if few else eng[d]))
+            tr.append(RemoteDMATransfer(dst_ids=[DstId(rid=rid, pnc=pid)], dma_engine_mask=m, remote_sem=T.sem[sem], src=src(d), dst=dst(d)))
+            total["lsent"] = total.get("lsent", 0) + (KE if few else len(eng[d]))
+        g.remote_dma_fused(tr, local_sem=T.sem.lsent)
+
+    t_kl = dma("y", [], T.kl[:], T.ky[:], "dkl")
+    for a in range(8):
+        t_lk = dma("ys"[a % 2], [], T.lki[16 * a:16 * a + 16, :], T.ky[:], "dlk")
+    for a in range(8):
+        t_sp = dma("ys"[a % 2], [], T.spi[16 * a:16 * a + 16, :], T.sp[:], "dsp")
+    dma("y", [], T.kcs[:].bitcast(dt.uint8), T.kc[:], "dk")
+    t_k = dma("s", [], T.kss[:], T.ks[:], "dk")
+    t_w = dma("y", [], T.wt[:], T.w[:], "dw")
+
+    def iota(name, pat, base, cm):
+        if SCRATCH[name][2] == I32:
+            return done(g.iota(T[name][:], pat, base, cm), "gi")
+        return done(g.iota(T[name][:], pat, base, cm, allow_small_or_imprecise_dtypes=True), "gi")
+    t_pi = iota("pidx", [[0, 1]], 0, 1)
+    t_ie = iota("i_exp", [[1, 16], [0, 2]], 0, 0)
+    t_is = iota("i_sel", [[32, 16]], 0, 0)
+    t_i3 = iota("i_e3", [[1, NB], [0, 2]], 0, 0)
+    t_id2 = iota("i_d2", [[16, 16]], NS, 0)
+    t_id3 = iota("i_d3", [[16, 24]], S, 0)
+    t_ivj = iota("i_vj", [[1, 16], [16, 16]], 0, 0)
+    low = [d for d in others if d < r]
+    if low:
+        need("g", [t_kl])
+        send(low, "kin", lambda d: T.kl[:], lambda d: T.kb[:, 4 * (r - d - 1):4 * (r - d)], True)
+    t_iv3 = iota("i_v3", [[32, 24], [1, 16]], Z0, 0)
+
+    vop([], "set", T.ones[:], 1.0)
+    vop([t_pi], "ts", T.pm[:, 0:1], T.pidx[:], 15, None, OP.bitwise_and)
+    vop([], "ts", T.pm[:, 1:2], T.pidx[:], 31, None, OP.bitwise_and)
+    vop([], "ts", T.pm[:, 2:3], T.pidx[:], 16, None, OP.bitwise_and)
+    t_pm = vop([], "ts", T.pm[:, 3:4], T.pidx[:], 5, None, OP.arith_shift_right)
+    t_pf = vop([t_pm], "copy", T.pf[:], T.pm[:])
+    t_ek = vop([t_ie], "copy", T.expk[:], T.i_exp[:])
+    vop([t_pf, t_is], "ts", T.sel[:], T.i_sel[:], T.pf[:, 1:2], None, OP.add)
+    t_six = vop([], "ts", T.tot[:], T.pf[:, 3:4], float(NB), None, OP.mult)
+    t_six = vop([t_six, t_i3], "ts", T.exp3[:], T.i_e3[:], T.tot[:], None, OP.add)
+    t_d2 = vop([t_id2], "ts", T.d2[:], T.i_d2[:], T.pf[:, 0:1], None, OP.add)
+    vop([t_d2], "ts", T.d2p[:], T.d2[:], 1.0, None, OP.add)
+    vop([t_id3], "ts", T.d3[:], T.i_d3[:], T.pf[:, 0:1], None, OP.add)
+    vop([], "set", T.zj[:], 0.0)
+    vop([], "set", T.st[:], 0.0)
+    vop([], "set", T.zo[:], 0.0)
+    t_lkf = vop([t_lk], "copy", T.lkf[:], T.lki[:])
+    t_at = vop([t_lkf], "tr", T.at[:], T.lkf[:])
+    t_xa = vop([t_at, t_ek], "copy", T.xa[:], T.at[:, 0:16].indirect(T.expk[:, 0:32]))
+    t_spf = vop([t_sp], "copy", T.spf[:], T.spi[:])
+    t_spx = vop([t_spf], "ts", T.spx[:], T.ones[:], T.spf[:], None, OP.mult)
+    t_fa = vop([t_xa], "tr", T.fa[:], T.xa[:])
+    t_spb = vop([t_spx], "tr", T.spb[:], T.spx[:])
+    vop([t_spb], "ts", T.r1[:], T.at[:, 0:16], T.spb[:, 0:1], float(SL), OP.is_ge, OP.mult)
+    vop([], "ts", T.r2[:], T.at[:, 0:16], T.spb[:, 1:2], float(SL), OP.is_ge, OP.mult)
+    t_r = vop([], "ts", T.r3[:], T.at[:, 0:16], T.spb[:, 2:3], float(SL), OP.is_ge, OP.mult)
+    t_r12 = vop([t_r], "tt", T.r12[:], T.r1[:], T.r2[:], OP.add)
+    t_fs = vop([t_fa], "copy", T.fs[:], T.fa[:].indirect(T.sel[:]))
+    t_rr = vop([t_r12], "tt", T.rr[:], T.r12[:], T.r3[:], OP.add)
+    t_vk = vop([t_fs], "ts", T.vk[:], T.fs[:], -1.0, BIG, OP.mult, OP.add)
+    t_h = vop([], "ts", T.e1[:, 0:1], T.pf[:, 2:3], 16.0, None, OP.mult)
+    t_vj = vop([t_ivj, t_h], "ts", T.vj[:], T.i_vj[:], T.e1[:, 0:1], None, OP.add)
+    vop([], "set", T.wk[:, 0:NS], 0.0)
+    t_fill = vop([], "set", T.wj[:, 0:NS], 0.0)
+
+    nl = N - 1 - r
+
+    def quads(tok, src, qu, qv, qo, n):
+        vop([tok], "tt", qu[0:32, 0:n], src[0:32, 0:n], src[32:64, 0:n], OP.add)
+        t = vop([], "tt", qv[0:32, 0:n], src[64:96, 0:n], src[96:128, 0:n], OP.add)
+        need("v", [t])
+        for b in range(4):
+            t = vop([], "tt", qo[32 * b:32 * b + 32, 0:n], qu[0:32, 0:n], qv[0:32, 0:n], OP.add)
+        return t
+
+    late = [None, None, None]
+
+    def fills():
+        vop([], "set", T.wo[:, 0:S], 0.0)
+        vop([t_iv3], "ts", T.v3[:], T.i_v3[:], T.pf[:, 2:3], None, OP.add)
+        vop([], "set", T.kf[:, 0:Z0], -1.0)
+        for s in range(N):
+            vop([], "set", T.kf[32:64, Z0 + SL * s:Z0 + SL * (s + 1)], float(s))
+            vop([], "set", T.kf[64:128, Z0 + SL * s:Z0 + SL * (s + 1)], float(s))
+        late[2] = vop([], "set", T.yw[:], 0.0)
+        t = vop([], "set", T.zt[:], 0.0)
+        t = vop([t], "q", T.zc[:], T.zs[:], T.zt[:])
+        dma("y", [t], T.fw[:, 0:Z0].bitcast(dt.uint8), T.zc[:, 0:Z0].bitcast(dt.uint8), "dz")
+        late[1] = dma("y", [t], T.fsc[:, 0:Z0], T.zs[:, 0:Z0], "dz")
+        late[0] = vop([t_w], "q", T.wq[:], T.wsc[:], T.wt[:])
+
+    if nl == 0:
+        t_f = vop([], "set", T.fl[:], 1.0)
+    else:
+        fills()
+        W = 128 * nl
+        need("v", [("kin", KE * nl)])
+        total["kin"] = KE * nl
+        t = vop([], "copy", T.x1[:, 0:W], T.kb[:, 0:4 * nl].indirect(T.expk[:, 0:8 * nl]))
+        t = vop([t], "tr", T.b1[:, 0:W], T.x1[:, 0:W])
+        t = vop([t], "copy", T.b1u[:, 0:W], T.b1[:, 0:W])
+        tc = []
+        for c in range(16):
+            tc.append(vop([t], "ts", T.cmp[:, W * c:W * (c + 1)], T.b1u[:, 0:W], T.at[:, c:c + 1], None, OP.is_equal))
+        ns = 7
+        for c in range(ns):
+            t_s = sop([tc[c]], T.js[:, W * c:W * (c + 1)], T.cmp[:, W * c:W * (c + 1)], AF.Copy, accum_out=T.rc[:, c:c + 1])
+        H = W // 2
+        for c in range(ns, 16):
+            t = vop([tc[c]], "scan", T.sc[:, H * c:H * (c + 1)], T.cmp[:, W * c:W * c + H], T.cmp[:, W * c + H:W * (c + 1)], 0.0, OP.add, OP.add)
+        t = vop([t], "copy", T.rc[:, ns:16], T.sc[:, H * (ns + 1) - 1:H * 16:H])
+        need("v", [t_s])
+        t = quads(t, T.rc, T.qu, T.qv, T.qo, 16)
+        t_f = vop([t], "ts", T.fl[:], T.qo[:], 0.0, None, OP.is_equal)
+
+    t_q = vop([t_f, t_rr, t_six], "scan", T.q0[:], T.rr[:], T.fl[:], 0.0, OP.max, OP.add)
+    t = vop([], "red", T.tot[:], T.fl[:], AxisListType.X, OP.add)
+    t_e = vop([t_vj], "tt", T.e1[:], T.d2p[:], T.fl[:], OP.mult)
+    vop([t_q], "ts", T.ct[:, 0:32], T.ones[:], T.q0[:, 15:16], None, OP.mult)
+    t = vop([t], "ts", T.ct[:, 32:64], T.ones[:], T.tot[:], None, OP.mult)
+    t2 = vop([t_e], "tt", T.e2[:], T.d2[:], T.e1[:], OP.subtract)
+    t = vop([t], "tr", T.ctt[:], T.ct[:])
+    t = vop([t], "scan", T.st[:, 1:33], T.ctt[:, 32:64], T.ctt[:, 0:32], 0.0, OP.add, OP.max)
+    t = vop([t], "tr", T.bt[:], T.st[:, 0:32])
+    t = vop([t], "scan", T.qq[:], T.rr[:], T.fl[:], T.bt[:, 0:1], OP.max, OP.add)
+    t = vop([t], "tt", T.o1[:], T.qq[:], T.fl[:], OP.mult)
+    t = vop([t, t2], "tt", T.o2[:], T.o1[:], T.e2[:], OP.add)
+    t_off = vop([t], "copy", T.off[:], T.o2[:])
+
+    t = vop([t_off, t_vk, t_fill], "copy", T.wk[:].indirect(T.off[:]), T.vk[:])
+    t = vop([t], "tr", T.tk[:], T.wk[:, 0:NS])
+    t = vop([t], "tt", T.zk[:], T.tk[:, 0:NS:32], T.tk[:, 16:NS:32], OP.add)
+    t_kz = vop([t], "ts", T.kz[:], T.zk[:], -1.0, BIG, OP.mult, OP.add)
+    need("g", [t_kz])
+    send(others, "slk", lambda d: T.kz[:, NB * d:NB * (d + 1)], lambda d: T.ap[:, NB * r:NB * (r + 1)], True)
+    t_own = dma("y", [t_kz], T.ap[:, NB * r:NB * (r + 1)], T.kz[:, NB * r:NB * (r + 1)], "own")
+
+    def lists(tok, z, s1, s2, s3, out, n):
+        t = vop([tok], "tr", s1[:], z[:])
+        need("v", [t])
+        for i in range(4):
+            t = vop([], "copy", s2[:, 16 * i:16 * i + 16], s1[:, 16 * (i // 2):16 * (i // 2) + 16])
+        t = vop([t], "tr", s3[:], s2[:])
+        vop([t], "copy", out[:, 0:2 * n:2], s3[:, 0:n])
+        return vop([], "copy", out[:, 1:2 * n:2], s3[:, 32:32 + n])
+
+    t = vop([t_off, t_vj], "copy", T.wj[:].indirect(T.off[:]), T.vj[:])
+    t = vop([t], "tr", T.tj[:], T.wj[:, 0:NS])
+    t = vop([t], "tt", T.zj[:, 0:24], T.tj[:, 0:NS:32], T.tj[:, 16:NS:32], OP.add)
+    t_lj = lists(t, T.zj, T.sw1, T.sw2, T.sw3, T.lj, 24)
+
+    for d in far + near + [r]:
+        L = T.lj[:, 12 * d:12 * d + CAPP // 16]
+        a = Z0 + SL * r
+        if d == r:
+            oc, osc = T.fw[:, a:a + CAPP], T.fsc[:, a:a + CAPP]
+        else:
+            oc, osc = T["pc%d" % d][:], T["ps%d" % d][:]
+        tv = vop([t_lj, t_k], "copy", oc.bitcast(dt.uint32), T.kcs[:].bitcast(dt.uint32).indirect(L))
+        ts = sop([t_lj, t_k], osc, T.kss[:].indirect(L), AF.Copy)
+        if d != r:
+            t_pv, t_ps = tv, ts
+    t_ov, t_os = tv, ts
+    a = Z0 + SL * r
+    need("g", [t_pv])
+    send(far + near, "colc", lambda d: T["pc%d" % d][:].bitcast(dt.uint8), lambda d: T.fw[:, a:a + CAPP].bitcast(dt.uint8), False)
+    need("g", [t_ps])
+    send(far + near, "cols", lambda d: T["ps%d" % d][:], lambda d: T.fsc[:, a:a + CAPP], False)
+    if nl == 0:
+        fills()
+
+    total["slk"] = KE * (N - 1)
+    total["colc"] = total["cols"] = sum(len(eng[d]) for d in others)
+    t_in = [("slk", total["slk"]), t_own]
+    t = vop(t_in, "copy", T.x3[:], T.ap[:].indirect(T.exp3[:]))
+    t_vm = vop([], "ts", T.vm[:], T.ap[:], 65536.0, None, OP.is_lt)
+    t_b3 = vop([t], "tr", T.b3[:], T.x3[:])
+    t_vd1 = vop([t_vm], "tt", T.vd1[:], T.d3[:], T.vm[:], OP.mult)
+    t = vop([t_b3], "copy", T.b3u[:], T.b3[:])
+    vop([t_vd1, t], "tt", T.vd[:], T.d3[:], T.vd1[:], OP.subtract)
+    ns = 9
+    for x in range(ns):
+        t_s = sop(t_in + [t_b3], T.j3[:, SL * x:SL * (x + 1)], T.b3[:], AF.Sign, bias=T.ap[:, x:x + 1], scale=-1.0, accum_out=T.rs3[:, x:x + 1])
+    for s in range(N):
+        sop([late[2]], T.kf[0:32, Z0 + SL * s:Z0 + SL * (s + 1)], T.b3[32 * s:32 * s + 32, :], AF.Copy)
+    for s in [r] + others:
+        a = Z0 + SL * s
+        dep = [t_ov, t_os] if s == r else [("colc", total["colc"]), ("cols", total["cols"])]
+        need("t", [late[0]] + dep)
+        t_t = done(g.tensor.matmul_mx(T.pz[:, 512 * s:512 * s + CAPP], T.wq[:], T.wsc[:], T.fw[:, a:a + CAPP], T.fsc[:, a:a + CAPP], True, True), "t")
+        t_y = sop([t_t, late[2]], T.yw[:, a:a + CAPP], T.pz[:, 512 * s:512 * s + CAPP], AF.Copy)
+    H = SL // 2
+    for x in range(ns, 24):
+        t = vop([], "ts", T.cmp3[:, SL * x:SL * (x + 1)], T.b3u[:], T.ap[:, x:x + 1], None, OP.is_lt)
+    need("v", [t])
+    for x in range(ns, 24):
+        t = vop([], "scan", T.sc3[:, H * x:H * (x + 1)], T.cmp3[:, SL * x:SL * x + H], T.cmp3[:, SL * x + H:SL * (x + 1)], 0.0, OP.add, OP.add)
+    t = vop([t], "copy", T.rc3[:, ns:24], T.sc3[:, H * (ns + 1) - 1:H * 24:H])
+    t = vop([t_s], "ts", T.rc3[:, 0:ns], T.rs3[:, 0:ns], 0.5, SL / 2 - 0.125, OP.mult, OP.add)
+    t = quads(t, T.rc3, T.qu3, T.qv3, T.qo3, 24)
+    t = vop([t], "tt", T.p1[:], T.qo3[:], T.vm[:], OP.mult)
+    t = vop([t], "tt", T.p2[:], T.p1[:], T.vd[:], OP.add)
+    t = vop([t], "copy", T.off3[:], T.p2[:])
+    t = vop([t], "copy", T.wo[:].indirect(T.off3[:]), T.v3[:])
+    t = vop([t], "tr", T.to[:], T.wo[:, 0:S])
+    t = vop([t], "tt", T.zo[:, 0:20], T.to[:, 0:S:32], T.to[:, 16:S:32], OP.add)
+    t_lf = lists(t, T.zo, T.so1, T.so2, T.so3, T.lf, 20)
+
+    t = sop([t_lf, ("cols", total["cols"]), t_os, late[1]], T.os_[:], T.fsc[:].indirect(T.lf[:]), AF.Copy)
+    for i in range(4):
+        dma("s", [t], T.osc[4 * i:4 * i + 4, :], T.os_[32 * i:32 * i + 4, :], "st2")
+    for c in range(S // CH):
+        lo, hi = c * CH, (c + 1) * CH
+        t = vop([t_lf, ("colc", total["colc"]), t_ov, late[1]], "copy", T.oq[:, lo:hi].bitcast(dt.uint32), T.fw[:].bitcast(dt.uint32).indirect(T.lf[:, lo // 16:hi // 16]))
+        dma("y", [t], T.oc[:, 4 * lo:4 * hi], T.oq[:, lo:hi].bitcast(dt.uint8), "st1")
+    for c in range(S // CH):
+        lo, hi = c * CH, (c + 1) * CH
+        t = vop([t_y], "copy", T.ys[:, lo:hi], T.yw[:].indirect(T.lf[:, lo // 16:hi // 16]))
+        dma("y", [t], T.y[:, lo:hi], T.ys[:, lo:hi], "st1")
+    t = sop([], T.okf[:], T.kf[:].indirect(T.lf[:]), AF.Copy)
+    dma("s", [t], T.ok[0:1, :], T.okf[0:1, :], "st2")
+    dma("s", [], T.ok[1:2, :], T.okf[32:33, :], "st2")
+    need("g", list(total.items()))

@@ -8,6 +8,8 @@ NS = N * SL
 Z0 = 32
 BIG = 70000.0
 CH = 320
+A1, A3 = 9, 12
+M1, M3 = 16 - A1, 24 - A3
 
 
 def _s(n, d="float32"):
@@ -17,21 +19,22 @@ def _s(n, d="float32"):
 X4, U8, U16, BF, I32 = "float8_e4m3fn_x4", "uint8", "uint16", "bfloat16", "int32"
 SCRATCH = {
     "kl": _s(4, I32), "lki": _s(32, I32), "spi": _s(1, I32), "wt": _s(512, BF), "kcs": _s(C, X4), "kss": _s(C, U8),
-    "pidx": _s(1, I32), "pm": _s(4, I32), "pf": _s(4), "ones": _s(32), "i_exp": _s(32, I32), "expk": _s(32, U16),
-    "i_sel": _s(16), "sel": _s(16, U16), "i_e3": _s(12), "exp3": _s(12, U16), "i_d2": _s(16), "d2": _s(16), "i_d3": _s(24), "d3": _s(24),
-    "i_vj": _s(256), "vj": _s(256), "i_v3": _s(384), "v3": _s(384), "zt": _s(512, BF), "zc": _s(128, X4), "zs": _s(128, U8), "d2p": _s(16),
+    "pidx": _s(1, I32), "pm": _s(6, I32), "pf": _s(6), "six": _s(1), "v32": _s(1), "vhf": _s(1), "vsum": _s(1), "ones": _s(32),
+    "i_exp": _s(32, I32), "expk": _s(32, U16), "i_sel": _s(16), "sel": _s(16, U16), "i_e3": _s(12), "exp3": _s(12, U16),
+    "i_dup": _s(4), "dup": _s(4, U16), "i_il": _s(3), "il": _s(3, U16), "d2": _s(16), "d2p": _s(16), "i_d3": _s(24), "d3": _s(24),
+    "i_vj": _s(256), "cj": _s(256), "i_v3": _s(384), "v3": _s(384), "zt": _s(512, BF), "zc": _s(128, X4), "zs": _s(128, U8),
     "lkf": _s(32), "at": _s(32), "spf": _s(1), "spx": _s(32), "spb": _s(32), "r1": _s(16), "r2": _s(16), "r3": _s(16), "r12": _s(16), "rr": _s(16),
     "xa": _s(512), "fa": _s(512), "fs": _s(256), "vk": _s(256),
-    "kb": _s(12, I32), "x1": _s(384), "b1": _s(384), "b1u": _s(384, U16), "cmp": _s(16 * 384, BF), "sc": _s(16 * 192, BF), "js": _s(8 * 384, BF),
-    "rc": _s(16), "qu": _s(16), "qv": _s(16), "qo": _s(16), "fl": _s(16),
+    "kb": _s(12, I32), "x1": _s(384), "b1": _s(384), "b1u": _s(384, U16), "cmp": _s(16 * 384, BF), "sc": _s(M1 * 192 + 1, BF), "js": _s(A1 * 384, BF),
+    "rc": _s(17), "qu": _s(24), "qo": _s(17), "fl": _s(16),
     "q0": _s(16), "tot": _s(1), "ct": _s(64), "ctt": _s(64), "st": _s(64), "bt": _s(32), "qq": _s(16), "e1": _s(16), "e2": _s(16), "o1": _s(16), "o2": _s(16), "off": _s(16, U16),
-    "wk": _s(NS + 256), "wj": _s(NS + 256), "tk": _s(NS), "tj": _s(NS), "zk": _s(24), "kz": _s(24), "zj": _s(32),
+    "wk": _s(NS + 256), "tk": _s(NS), "zi": _s(24, I32), "ki": _s(24, I32), "ji": _s(24, I32), "bz": _s(24), "ho": _s(24), "kz": _s(24), "zj": _s(32),
     "sw1": _s(32), "sw2": _s(64), "sw3": _s(64), "lj": _s(48, U16),
     "pc0": _s(CAPP, X4), "pc1": _s(CAPP, X4), "pc2": _s(CAPP, X4), "pc3": _s(CAPP, X4),
     "ps0": _s(CAPP, U8), "ps1": _s(CAPP, U8), "ps2": _s(CAPP, U8), "ps3": _s(CAPP, U8),
-    "ap": _s(24), "x3": _s(SL), "b3": _s(SL), "b3u": _s(SL, U16), "cmp3": _s(24 * SL, BF), "sc3": _s(24 * SL // 2, BF), "j3": _s(24 * SL, BF), "rs3": _s(24),
-    "rc3": _s(24), "qu3": _s(24), "qv3": _s(24), "qo3": _s(24), "vm": _s(24), "vd1": _s(24), "vd": _s(24), "p1": _s(24), "p2": _s(24), "off3": _s(24, U16),
-    "wo": _s(S + 384), "to": _s(S), "zo": _s(32), "so1": _s(32), "so2": _s(64), "so3": _s(64), "lf": _s(40, U16),
+    "ap": _s(24), "x3": _s(SL), "b3": _s(SL), "b3u": _s(SL, U16), "cmp3": _s(24 * SL, BF), "sc3": _s(M3 * SL // 2 + 1), "j3": _s(A3 * SL, BF), "rs3": _s(24),
+    "rc3": _s(24), "qu3": _s(24), "qo3": _s(24), "vm": _s(24), "vd1": _s(24), "vd": _s(24), "p1": _s(24), "p2": _s(24), "off3": _s(24, U16),
+    "wo": _s(S + 384), "to": _s(S), "zo": _s(32), "so1": _s(32), "so2": _s(64), "so3": _s(64), "lf": _s(48, U16),
     "fw": _s(Z0 + NS, X4), "fsc": _s(Z0 + NS, U8), "oq": _s(S, X4), "os_": _s(S, U8), "wq": _s(128, X4), "wsc": _s(128, U8),
     "kf": _s(Z0 + NS), "okf": _s(S), "yw": _s(Z0 + NS), "ys": _s(S), "pz": ("psum", [128, 512 * N], "float32"),
 }
@@ -76,11 +79,10 @@ def rank_program(g, core, T, topo):
     far = [d for d in others if topo.chip(T.cores[d]) != topo.chip(core)]
     near = [d for d in others if d not in far]
     fe = topo.engines(core, T.cores[far[0]])
-    k = len(fe) // len(far)
-    eng = {d: fe[i * k:(i + 1) * k] for i, d in enumerate(far)}
+    KE = len(fe) // len(far)
+    eng = {d: fe[i * KE:(i + 1) * KE] for i, d in enumerate(far)}
     for d in near:
         eng[d] = [e for e in topo.engines(core, T.cores[d]) if e not in fe]
-    KE = k
 
     def send(dests, sem, src, dst, few):
         tr = []
@@ -97,116 +99,108 @@ def rank_program(g, core, T, topo):
     for a in range(8):
         t_sp = dma("ys"[a % 2], [], T.spi[16 * a:16 * a + 16, :], T.sp[:], "dsp")
     dma("y", [], T.kcs[:].bitcast(dt.uint8), T.kc[:], "dk")
-    t_k = dma("s", [], T.kss[:], T.ks[:], "dk")
+    t_k = dma("y", [], T.kss[:], T.ks[:], "dk")
     t_w = dma("y", [], T.wt[:], T.w[:], "dw")
 
-    def iota(name, pat, base, cm):
-        if SCRATCH[name][2] == I32:
-            return done(g.iota(T[name][:], pat, base, cm), "gi")
-        return done(g.iota(T[name][:], pat, base, cm, allow_small_or_imprecise_dtypes=True), "gi")
-    t_pi = iota("pidx", [[0, 1]], 0, 1)
-    t_ie = iota("i_exp", [[1, 16], [0, 2]], 0, 0)
-    t_is = iota("i_sel", [[32, 16]], 0, 0)
-    t_i3 = iota("i_e3", [[1, NB], [0, 2]], 0, 0)
-    t_id2 = iota("i_d2", [[16, 16]], NS, 0)
-    t_id3 = iota("i_d3", [[16, 24]], S, 0)
-    t_ivj = iota("i_vj", [[1, 16], [16, 16]], 0, 0)
+    def iota(out, pat, base, cm=0, i32=False):
+        if i32:
+            return done(g.iota(out, pat, base, cm), "gi")
+        return done(g.iota(out, pat, base, cm, allow_small_or_imprecise_dtypes=True), "gi")
+    t_pi = iota(T.pidx[:], [[0, 1]], 0, 1, True)
+    t_ie = iota(T.i_exp[:], [[1, 16], [0, 2]], 0, 0, True)
+    iota(T.i_sel[:], [[32, 16]], 0)
+    iota(T.i_e3[:], [[1, NB], [0, 2]], 0)
+    iota(T.i_dup[:], [[16, 2], [0, 2]], 0)
+    iota(T.i_il[:], [[8, 3]], 0)
+    t_ic = iota(T.i_d3[:], [[16, 24]], S)
     low = [d for d in others if d < r]
     if low:
         need("g", [t_kl])
         send(low, "kin", lambda d: T.kl[:], lambda d: T.kb[:, 4 * (r - d - 1):4 * (r - d)], True)
-    t_iv3 = iota("i_v3", [[32, 24], [1, 16]], Z0, 0)
+    t_ivj = iota(T.i_vj[:], [[1, 16], [16, 16]], 0)
+    t_wk = iota(T.wk[:, 0:NS], [[0, NS]], -1)
+    t_iv3 = iota(T.i_v3[:], [[32, 24], [1, 16]], Z0)
+    iota(T.kf[:, 0:Z0], [[0, Z0]], -1)
+    t_kf = iota(T.kf[:, Z0:Z0 + NS], [[1, N], [0, SL]], 0)
+    t_yw = iota(T.yw[:], [[0, Z0 + NS]], 0)
+    t_wo = iota(T.wo[:, 0:S], [[0, S]], 0)
 
     vop([], "set", T.ones[:], 1.0)
-    vop([t_pi], "ts", T.pm[:, 0:1], T.pidx[:], 15, None, OP.bitwise_and)
-    vop([], "ts", T.pm[:, 1:2], T.pidx[:], 31, None, OP.bitwise_and)
-    vop([], "ts", T.pm[:, 2:3], T.pidx[:], 16, None, OP.bitwise_and)
-    t_pm = vop([], "ts", T.pm[:, 3:4], T.pidx[:], 5, None, OP.arith_shift_right)
-    t_pf = vop([t_pm], "copy", T.pf[:], T.pm[:])
+    for name in ("zj", "st", "zo"):
+        vop([], "set", T[name][:], 0.0)
+    vop([], "set", T.sc3[:, 0:1], 0.0)
+    vop([], "set", T.sc[:, 0:1], 0.0)
+    t_zt = vop([], "set", T.zt[:], 0.0)
+    need("v", [t_pi])
+    for i, b in enumerate((15, 31, 16, 1, 14)):
+        vop([], "ts", T.pm[:, i:i + 1], T.pidx[:], b, None, OP.bitwise_and)
+    t = vop([], "ts", T.pm[:, 5:6], T.pidx[:], 5, None, OP.arith_shift_right)
+    t_pf = vop([t], "copy", T.pf[:], T.pm[:])
     t_ek = vop([t_ie], "copy", T.expk[:], T.i_exp[:])
-    vop([t_pf, t_is], "ts", T.sel[:], T.i_sel[:], T.pf[:, 1:2], None, OP.add)
-    t_six = vop([], "ts", T.tot[:], T.pf[:, 3:4], float(NB), None, OP.mult)
-    t_six = vop([t_six, t_i3], "ts", T.exp3[:], T.i_e3[:], T.tot[:], None, OP.add)
-    t_d2 = vop([t_id2], "ts", T.d2[:], T.i_d2[:], T.pf[:, 0:1], None, OP.add)
+    need("v", [t_pf, t_ic])
+    vop([], "ts", T.six[:], T.pf[:, 5:6], float(NB), None, OP.mult)
+    vop([], "ts", T.v32[:], T.pf[:, 3:4], 32.0, None, OP.mult)
+    t = vop([], "ts", T.vhf[:], T.pf[:, 4:5], 0.5, None, OP.mult)
+    t_sel = vop([], "ts", T.sel[:], T.i_sel[:], T.pf[:, 1:2], None, OP.add)
+    vop([], "ts", T.dup[:], T.i_dup[:], T.pf[:, 0:1], None, OP.add)
+    vop([], "ts", T.d3[:], T.i_d3[:], T.pf[:, 0:1], None, OP.add)
+    t_d2 = vop([], "ts", T.d2[:], T.i_d3[:, 0:16], T.pf[:, 0:1], float(NS - S), OP.add, OP.add)
+    t = vop([t], "ts", T.vsum[:], T.v32[:], T.vhf[:], None, OP.add)
+    vop([], "ts", T.exp3[:], T.i_e3[:], T.six[:], None, OP.add)
     vop([t_d2], "ts", T.d2p[:], T.d2[:], 1.0, None, OP.add)
-    vop([t_id3], "ts", T.d3[:], T.i_d3[:], T.pf[:, 0:1], None, OP.add)
-    vop([], "set", T.zj[:], 0.0)
-    vop([], "set", T.st[:], 0.0)
-    vop([], "set", T.zo[:], 0.0)
+    t_c = vop([t], "ts", T.il[:], T.i_il[:], T.vsum[:], None, OP.add)
     t_lkf = vop([t_lk], "copy", T.lkf[:], T.lki[:])
     t_at = vop([t_lkf], "tr", T.at[:], T.lkf[:])
-    t_xa = vop([t_at, t_ek], "copy", T.xa[:], T.at[:, 0:16].indirect(T.expk[:, 0:32]))
+    t_xa = sop([t_at, t_ek], T.xa[:], T.at[:, 0:16].indirect(T.expk[:]), AF.Copy)
     t_spf = vop([t_sp], "copy", T.spf[:], T.spi[:])
     t_spx = vop([t_spf], "ts", T.spx[:], T.ones[:], T.spf[:], None, OP.mult)
-    t_fa = vop([t_xa], "tr", T.fa[:], T.xa[:])
     t_spb = vop([t_spx], "tr", T.spb[:], T.spx[:])
     vop([t_spb], "ts", T.r1[:], T.at[:, 0:16], T.spb[:, 0:1], float(SL), OP.is_ge, OP.mult)
-    vop([], "ts", T.r2[:], T.at[:, 0:16], T.spb[:, 1:2], float(SL), OP.is_ge, OP.mult)
-    t_r = vop([], "ts", T.r3[:], T.at[:, 0:16], T.spb[:, 2:3], float(SL), OP.is_ge, OP.mult)
+    t_r = vop([], "ts", T.r2[:], T.at[:, 0:16], T.spb[:, 1:2], float(SL), OP.is_ge, OP.mult)
+    t_r3 = vop([], "ts", T.r3[:], T.at[:, 0:16], T.spb[:, 2:3], float(SL), OP.is_ge, OP.mult)
     t_r12 = vop([t_r], "tt", T.r12[:], T.r1[:], T.r2[:], OP.add)
-    t_fs = vop([t_fa], "copy", T.fs[:], T.fa[:].indirect(T.sel[:]))
-    t_rr = vop([t_r12], "tt", T.rr[:], T.r12[:], T.r3[:], OP.add)
-    t_vk = vop([t_fs], "ts", T.vk[:], T.fs[:], -1.0, BIG, OP.mult, OP.add)
-    t_h = vop([], "ts", T.e1[:, 0:1], T.pf[:, 2:3], 16.0, None, OP.mult)
-    t_vj = vop([t_ivj, t_h], "ts", T.vj[:], T.i_vj[:], T.e1[:, 0:1], None, OP.add)
-    vop([], "set", T.wk[:, 0:NS], 0.0)
-    t_fill = vop([], "set", T.wj[:, 0:NS], 0.0)
+    t_rr = vop([t_r12, t_r3], "tt", T.rr[:], T.r12[:], T.r3[:], OP.add)
+    t_fa = vop([t_xa], "tr", T.fa[:], T.xa[:])
+    t_fs = sop([t_fa, t_sel], T.fs[:], T.fa[:].indirect(T.sel[:]), AF.Copy)
+    t_cj = vop([t_ivj], "ts", T.cj[:], T.i_vj[:], 65536.0, 1.0, OP.mult, OP.add)
+    t_vk = vop([t_cj, t_fs], "tt", T.vk[:], T.fs[:], T.cj[:], OP.add)
 
     nl = N - 1 - r
 
-    def quads(tok, src, qu, qv, qo, n):
-        vop([tok], "tt", qu[0:32, 0:n], src[0:32, 0:n], src[32:64, 0:n], OP.add)
-        t = vop([], "tt", qv[0:32, 0:n], src[64:96, 0:n], src[96:128, 0:n], OP.add)
+    def quads(tok, src, qu, qo, n):
+        t = vop([tok], "tt", qu[0:64, 0:n], src[0:64, 0:n], src[64:128, 0:n], OP.add)
         need("v", [t])
         for b in range(4):
-            t = vop([], "tt", qo[32 * b:32 * b + 32, 0:n], qu[0:32, 0:n], qv[0:32, 0:n], OP.add)
+            t = vop([], "tt", qo[32 * b:32 * b + 32, 0:n], qu[0:32, 0:n], qu[32:64, 0:n], OP.add)
         return t
-
-    late = [None, None, None]
-
-    def fills():
-        vop([], "set", T.wo[:, 0:S], 0.0)
-        vop([t_iv3], "ts", T.v3[:], T.i_v3[:], T.pf[:, 2:3], None, OP.add)
-        vop([], "set", T.kf[:, 0:Z0], -1.0)
-        for s in range(N):
-            vop([], "set", T.kf[32:64, Z0 + SL * s:Z0 + SL * (s + 1)], float(s))
-            vop([], "set", T.kf[64:128, Z0 + SL * s:Z0 + SL * (s + 1)], float(s))
-        late[2] = vop([], "set", T.yw[:], 0.0)
-        t = vop([], "set", T.zt[:], 0.0)
-        t = vop([t], "q", T.zc[:], T.zs[:], T.zt[:])
-        dma("y", [t], T.fw[:, 0:Z0].bitcast(dt.uint8), T.zc[:, 0:Z0].bitcast(dt.uint8), "dz")
-        late[1] = dma("y", [t], T.fsc[:, 0:Z0], T.zs[:, 0:Z0], "dz")
-        late[0] = vop([t_w], "q", T.wq[:], T.wsc[:], T.wt[:])
 
     if nl == 0:
         t_f = vop([], "set", T.fl[:], 1.0)
     else:
-        fills()
         W = 128 * nl
-        need("v", [("kin", KE * nl)])
-        total["kin"] = KE * nl
-        t = vop([], "copy", T.x1[:, 0:W], T.kb[:, 0:4 * nl].indirect(T.expk[:, 0:8 * nl]))
-        t = vop([t], "tr", T.b1[:, 0:W], T.x1[:, 0:W])
-        t = vop([t], "copy", T.b1u[:, 0:W], T.b1[:, 0:W])
-        tc = []
-        for c in range(16):
-            tc.append(vop([t], "ts", T.cmp[:, W * c:W * (c + 1)], T.b1u[:, 0:W], T.at[:, c:c + 1], None, OP.is_equal))
-        ns = 7
-        for c in range(ns):
-            t_s = sop([tc[c]], T.js[:, W * c:W * (c + 1)], T.cmp[:, W * c:W * (c + 1)], AF.Copy, accum_out=T.rc[:, c:c + 1])
         H = W // 2
-        for c in range(ns, 16):
-            t = vop([tc[c]], "scan", T.sc[:, H * c:H * (c + 1)], T.cmp[:, W * c:W * c + H], T.cmp[:, W * c + H:W * (c + 1)], 0.0, OP.add, OP.add)
-        t = vop([t], "copy", T.rc[:, ns:16], T.sc[:, H * (ns + 1) - 1:H * 16:H])
+        total["kin"] = KE * nl
+        t_kin = ("kin", KE * nl)
+        t2 = sop([t_kin, t_ek], T.x1[:, H:W], T.kb[:, 0:4 * nl].indirect(T.expk[:, 4 * nl:8 * nl]), AF.Copy)
+        t = vop([t_kin], "copy", T.x1[:, 0:H], T.kb[:, 0:4 * nl].indirect(T.expk[:, 0:4 * nl]))
+        t = vop([t, t2], "tr", T.b1[:, 0:W], T.x1[:, 0:W])
+        t = vop([t], "copy", T.b1u[:, 0:W], T.b1[:, 0:W])
+        for c in range(16):
+            t = vop([t] if c == 0 else [], "ts", T.cmp[:, W * c:W * (c + 1)], T.b1u[:, 0:W], T.at[:, c:c + 1], None, OP.is_equal)
+            if c < A1:
+                t_s = sop([t], T.js[:, W * c:W * (c + 1)], T.cmp[:, W * c:W * (c + 1)], AF.Copy, accum_out=T.rc[:, c:c + 1])
+        t = vop([t], "scan", T.sc[:, 1:M1 * H + 1], T.cmp[:, A1 * W:16 * W:2], T.cmp[:, A1 * W + 1:16 * W:2], 0.0, OP.add, OP.add)
+        t = vop([t], "copy", T.rc[:, A1:17], T.sc[:, 0:M1 * H + 1:H])
         need("v", [t_s])
-        t = quads(t, T.rc, T.qu, T.qv, T.qo, 16)
-        t_f = vop([t], "ts", T.fl[:], T.qo[:], 0.0, None, OP.is_equal)
+        t = quads(t, T.rc, T.qu, T.qo, 17)
+        vop([t], "ts", T.fl[:, 0:A1], T.qo[:, 0:A1], 0.0, None, OP.is_equal)
+        t_f = vop([], "tt", T.fl[:, A1:16], T.qo[:, A1 + 1:17], T.qo[:, A1:16], OP.is_equal)
 
-    t_q = vop([t_f, t_rr, t_six], "scan", T.q0[:], T.rr[:], T.fl[:], 0.0, OP.max, OP.add)
-    t = vop([], "red", T.tot[:], T.fl[:], AxisListType.X, OP.add)
-    t_e = vop([t_vj], "tt", T.e1[:], T.d2p[:], T.fl[:], OP.mult)
+    t_tot = sop([t_f], T.js[:, 0:16], T.fl[:], AF.Copy, accum_out=T.tot[:])
+    t_q = vop([t_f, t_rr], "scan", T.q0[:], T.rr[:], T.fl[:], 0.0, OP.max, OP.add)
+    t_e = vop([t_c], "tt", T.e1[:], T.d2p[:], T.fl[:], OP.mult)
     vop([t_q], "ts", T.ct[:, 0:32], T.ones[:], T.q0[:, 15:16], None, OP.mult)
-    t = vop([t], "ts", T.ct[:, 32:64], T.ones[:], T.tot[:], None, OP.mult)
+    t = vop([t_tot], "ts", T.ct[:, 32:64], T.ones[:], T.tot[:], None, OP.mult)
     t2 = vop([t_e], "tt", T.e2[:], T.d2[:], T.e1[:], OP.subtract)
     t = vop([t], "tr", T.ctt[:], T.ct[:])
     t = vop([t], "scan", T.st[:, 1:33], T.ctt[:, 32:64], T.ctt[:, 0:32], 0.0, OP.add, OP.max)
@@ -216,47 +210,50 @@ def rank_program(g, core, T, topo):
     t = vop([t, t2], "tt", T.o2[:], T.o1[:], T.e2[:], OP.add)
     t_off = vop([t], "copy", T.off[:], T.o2[:])
 
-    t = vop([t_off, t_vk, t_fill], "copy", T.wk[:].indirect(T.off[:]), T.vk[:])
+    t = vop([t_off, t_vk, t_wk], "copy", T.wk[:].indirect(T.off[:]), T.vk[:])
     t = vop([t], "tr", T.tk[:], T.wk[:, 0:NS])
-    t = vop([t], "tt", T.zk[:], T.tk[:, 0:NS:32], T.tk[:, 16:NS:32], OP.add)
-    t_kz = vop([t], "ts", T.kz[:], T.zk[:], -1.0, BIG, OP.mult, OP.add)
+    te, to = T.tk[:, 0:NS:32], T.tk[:, 16:NS:32]
+    t_zi = vop([t], "tt", T.zi[:], te, to, OP.add)
+    vop([t_zi], "ts", T.ki[:], T.zi[:], 65535, None, OP.bitwise_and)
+    t = vop([], "ts", T.bz[:], T.zi[:], 0.0, BIG, OP.is_lt, OP.mult)
+    t_kz = vop([t], "tt", T.kz[:], T.ki[:], T.bz[:], OP.add)
     need("g", [t_kz])
     send(others, "slk", lambda d: T.kz[:, NB * d:NB * (d + 1)], lambda d: T.ap[:, NB * r:NB * (r + 1)], True)
     t_own = dma("y", [t_kz], T.ap[:, NB * r:NB * (r + 1)], T.kz[:, NB * r:NB * (r + 1)], "own")
 
-    def lists(tok, z, s1, s2, s3, out, n):
+    def lists(tok, z, s1, s2, s3, out):
         t = vop([tok], "tr", s1[:], z[:])
-        need("v", [t])
-        for i in range(4):
-            t = vop([], "copy", s2[:, 16 * i:16 * i + 16], s1[:, 16 * (i // 2):16 * (i // 2) + 16])
+        t = vop([t], "copy", s2[:], s1[:].indirect(T.dup[:]))
         t = vop([t], "tr", s3[:], s2[:])
-        vop([t], "copy", out[:, 0:2 * n:2], s3[:, 0:n])
-        return vop([], "copy", out[:, 1:2 * n:2], s3[:, 32:32 + n])
+        return vop([t], "copy", out[:], s3[:].indirect(T.il[:]))
 
-    t = vop([t_off, t_vj], "copy", T.wj[:].indirect(T.off[:]), T.vj[:])
-    t = vop([t], "tr", T.tj[:], T.wj[:, 0:NS])
-    t = vop([t], "tt", T.zj[:, 0:24], T.tj[:, 0:NS:32], T.tj[:, 16:NS:32], OP.add)
-    t_lj = lists(t, T.zj, T.sw1, T.sw2, T.sw3, T.lj, 24)
+    vop([], "ts", T.ji[:], T.zi[:], 16, None, OP.arith_shift_right)
+    t = vop([], "ts", T.ho[:], to, 0.0, 256.0, OP.is_ge, OP.mult)
+    t = vop([t], "tt", T.zj[:, 0:24], T.ji[:], T.ho[:], OP.add)
+    t_lj = lists(t, T.zj, T.sw1, T.sw2, T.sw3, T.lj)
 
-    for d in far + near + [r]:
+    def pick(d, oc, osc):
         L = T.lj[:, 12 * d:12 * d + CAPP // 16]
-        a = Z0 + SL * r
-        if d == r:
-            oc, osc = T.fw[:, a:a + CAPP], T.fsc[:, a:a + CAPP]
-        else:
-            oc, osc = T["pc%d" % d][:], T["ps%d" % d][:]
-        tv = vop([t_lj, t_k], "copy", oc.bitcast(dt.uint32), T.kcs[:].bitcast(dt.uint32).indirect(L))
-        ts = sop([t_lj, t_k], osc, T.kss[:].indirect(L), AF.Copy)
-        if d != r:
-            t_pv, t_ps = tv, ts
-    t_ov, t_os = tv, ts
-    a = Z0 + SL * r
+        return (vop([t_lj, t_k], "copy", oc.bitcast(dt.uint32), T.kcs[:].bitcast(dt.uint32).indirect(L)),
+                sop([t_lj, t_k], osc, T.kss[:].indirect(L), AF.Copy))
+    for d in far + near:
+        t_pv, t_ps = pick(d, T["pc%d" % d][:], T["ps%d" % d][:])
+    w0 = Z0 + SL * r
     need("g", [t_pv])
-    send(far + near, "colc", lambda d: T["pc%d" % d][:].bitcast(dt.uint8), lambda d: T.fw[:, a:a + CAPP].bitcast(dt.uint8), False)
+    send(far + near, "colc", lambda d: T["pc%d" % d][:].bitcast(dt.uint8), lambda d: T.fw[:, w0:w0 + CAPP].bitcast(dt.uint8), False)
     need("g", [t_ps])
-    send(far + near, "cols", lambda d: T["ps%d" % d][:], lambda d: T.fsc[:, a:a + CAPP], False)
-    if nl == 0:
-        fills()
+    send(far + near, "cols", lambda d: T["ps%d" % d][:], lambda d: T.fsc[:, w0:w0 + CAPP], False)
+
+    tk = {}
+
+    def own():
+        tk["v"], tk["s"] = pick(r, T.fw[:, w0:w0 + CAPP], T.fsc[:, w0:w0 + CAPP])
+        t = vop([t_zt], "q", T.zc[:], T.zs[:], T.zt[:])
+        dma("y", [t], T.fw[:, 0:Z0].bitcast(dt.uint8), T.zc[:, 0:Z0].bitcast(dt.uint8), "dz")
+        tk["z"] = dma("y", [t], T.fsc[:, 0:Z0], T.zs[:, 0:Z0], "dz")
+        tk["w"] = vop([t_w], "q", T.wq[:], T.wsc[:], T.wt[:])
+    if r:
+        own()
 
     total["slk"] = KE * (N - 1)
     total["colc"] = total["cols"] = sum(len(eng[d]) for d in others)
@@ -264,49 +261,49 @@ def rank_program(g, core, T, topo):
     t = vop(t_in, "copy", T.x3[:], T.ap[:].indirect(T.exp3[:]))
     t_vm = vop([], "ts", T.vm[:], T.ap[:], 65536.0, None, OP.is_lt)
     t_b3 = vop([t], "tr", T.b3[:], T.x3[:])
-    t_vd1 = vop([t_vm], "tt", T.vd1[:], T.d3[:], T.vm[:], OP.mult)
-    t = vop([t_b3], "copy", T.b3u[:], T.b3[:])
-    vop([t_vd1, t], "tt", T.vd[:], T.d3[:], T.vd1[:], OP.subtract)
-    ns = 9
-    for x in range(ns):
+    for x in range(A3):
         t_s = sop(t_in + [t_b3], T.j3[:, SL * x:SL * (x + 1)], T.b3[:], AF.Sign, bias=T.ap[:, x:x + 1], scale=-1.0, accum_out=T.rs3[:, x:x + 1])
+    t = vop([t_b3], "copy", T.b3u[:], T.b3[:])
+    H = SL // 2
+    need("v", [t])
+    for x in range(A3, 24):
+        t = vop([], "ts", T.cmp3[:, SL * x:SL * (x + 1)], T.b3u[:], T.ap[:, x:x + 1], None, OP.is_lt)
+    t = vop([t], "scan", T.sc3[:, 1:M3 * H + 1], T.cmp3[:, A3 * SL:24 * SL:2], T.cmp3[:, A3 * SL + 1:24 * SL:2], 0.0, OP.add, OP.add)
+    t_vd = vop([t_vm], "tt", T.vd1[:], T.d3[:], T.vm[:], OP.mult)
+    t = vop([t], "tt", T.rc3[:, A3:24], T.sc3[:, H:M3 * H + 1:H], T.sc3[:, 0:(M3 - 1) * H + 1:H], OP.subtract)
+    vop([t_vd], "tt", T.vd[:], T.d3[:], T.vd1[:], OP.subtract)
+    if r == 0:
+        own()
+    t = vop([t_s], "ts", T.rc3[:, 0:A3], T.rs3[:, 0:A3], 0.5, SL / 2 - 0.125, OP.mult, OP.add)
+    t_v3 = sop([t_iv3, t_pf], T.v3[:], T.i_v3[:], AF.Identity, bias=T.pf[:, 2:3])
     for s in range(N):
-        sop([late[2]], T.kf[0:32, Z0 + SL * s:Z0 + SL * (s + 1)], T.b3[32 * s:32 * s + 32, :], AF.Copy)
+        t_kc = sop([t_kf], T.kf[0:32, Z0 + SL * s:Z0 + SL * (s + 1)], T.b3[32 * s:32 * s + 32, :], AF.Copy)
     for s in [r] + others:
         a = Z0 + SL * s
-        dep = [t_ov, t_os] if s == r else [("colc", total["colc"]), ("cols", total["cols"])]
-        need("t", [late[0]] + dep)
+        need("t", [tk["w"]] + ([tk["v"], tk["s"]] if s == r else [("colc", total["colc"]), ("cols", total["cols"])]))
         t_t = done(g.tensor.matmul_mx(T.pz[:, 512 * s:512 * s + CAPP], T.wq[:], T.wsc[:], T.fw[:, a:a + CAPP], T.fsc[:, a:a + CAPP], True, True), "t")
-        t_y = sop([t_t, late[2]], T.yw[:, a:a + CAPP], T.pz[:, 512 * s:512 * s + CAPP], AF.Copy)
-    H = SL // 2
-    for x in range(ns, 24):
-        t = vop([], "ts", T.cmp3[:, SL * x:SL * (x + 1)], T.b3u[:], T.ap[:, x:x + 1], None, OP.is_lt)
-    need("v", [t])
-    for x in range(ns, 24):
-        t = vop([], "scan", T.sc3[:, H * x:H * (x + 1)], T.cmp3[:, SL * x:SL * x + H], T.cmp3[:, SL * x + H:SL * (x + 1)], 0.0, OP.add, OP.add)
-    t = vop([t], "copy", T.rc3[:, ns:24], T.sc3[:, H * (ns + 1) - 1:H * 24:H])
-    t = vop([t_s], "ts", T.rc3[:, 0:ns], T.rs3[:, 0:ns], 0.5, SL / 2 - 0.125, OP.mult, OP.add)
-    t = quads(t, T.rc3, T.qu3, T.qv3, T.qo3, 24)
+        t_y = sop([t_t, t_yw], T.yw[:, a:a + CAPP], T.pz[:, 512 * s:512 * s + CAPP], AF.Copy)
+    t = quads(t, T.rc3, T.qu3, T.qo3, 24)
     t = vop([t], "tt", T.p1[:], T.qo3[:], T.vm[:], OP.mult)
     t = vop([t], "tt", T.p2[:], T.p1[:], T.vd[:], OP.add)
     t = vop([t], "copy", T.off3[:], T.p2[:])
-    t = vop([t], "copy", T.wo[:].indirect(T.off3[:]), T.v3[:])
+    t = vop([t, t_v3, t_wo], "copy", T.wo[:].indirect(T.off3[:]), T.v3[:])
     t = vop([t], "tr", T.to[:], T.wo[:, 0:S])
     t = vop([t], "tt", T.zo[:, 0:20], T.to[:, 0:S:32], T.to[:, 16:S:32], OP.add)
-    t_lf = lists(t, T.zo, T.so1, T.so2, T.so3, T.lf, 20)
+    t_lf = lists(t, T.zo, T.so1, T.so2, T.so3, T.lf)
 
-    t = sop([t_lf, ("cols", total["cols"]), t_os, late[1]], T.os_[:], T.fsc[:].indirect(T.lf[:]), AF.Copy)
-    for i in range(4):
-        dma("s", [t], T.osc[4 * i:4 * i + 4, :], T.os_[32 * i:32 * i + 4, :], "st2")
+    t_sc = sop([t_lf, ("cols", total["cols"]), tk["s"], tk["z"]], T.os_[:], T.fsc[:].indirect(T.lf[:, 0:S // 16]), AF.Copy)
     for c in range(S // CH):
         lo, hi = c * CH, (c + 1) * CH
-        t = vop([t_lf, ("colc", total["colc"]), t_ov, late[1]], "copy", T.oq[:, lo:hi].bitcast(dt.uint32), T.fw[:].bitcast(dt.uint32).indirect(T.lf[:, lo // 16:hi // 16]))
+        t = vop([t_lf, ("colc", total["colc"]), tk["v"], tk["z"]], "copy", T.oq[:, lo:hi].bitcast(dt.uint32), T.fw[:].bitcast(dt.uint32).indirect(T.lf[:, lo // 16:hi // 16]))
         dma("y", [t], T.oc[:, 4 * lo:4 * hi], T.oq[:, lo:hi].bitcast(dt.uint8), "st1")
+    for i in range(4):
+        dma("y", [t_sc], T.osc[4 * i:4 * i + 4, :], T.os_[32 * i:32 * i + 4, :], "st1")
     for c in range(S // CH):
         lo, hi = c * CH, (c + 1) * CH
         t = vop([t_y], "copy", T.ys[:, lo:hi], T.yw[:].indirect(T.lf[:, lo // 16:hi // 16]))
         dma("y", [t], T.y[:, lo:hi], T.ys[:, lo:hi], "st1")
-    t = sop([], T.okf[:], T.kf[:].indirect(T.lf[:]), AF.Copy)
+    t = sop([t_kc, t_lf], T.okf[:], T.kf[:].indirect(T.lf[:, 0:S // 16]), AF.Copy)
     dma("s", [t], T.ok[0:1, :], T.okf[0:1, :], "st2")
     dma("s", [], T.ok[1:2, :], T.okf[32:33, :], "st2")
     need("g", list(total.items()))

@@ -1,5 +1,5 @@
 from concourse.bass import DstId, RemoteDMATransfer
-from concourse.mybir import dt, AluOpType as OP, AxisListType, ActivationFunctionType as AF
+from concourse.mybir import dt, AluOpType as OP, ActivationFunctionType as AF
 
 N, C, S, CAPP = 4, 512, 640, 176
 SL = 192
@@ -8,8 +8,10 @@ NS = N * SL
 Z0 = 32
 BIG = 70000.0
 CH = 320
-A1, A3 = 9, 12
-M1, M3 = 16 - A1, 24 - A3
+YV = 384
+A3 = 11
+M3 = 24 - A3
+R0 = -float(M3 * SL // 2)
 
 
 def _s(n, d="float32"):
@@ -21,20 +23,20 @@ SCRATCH = {
     "kl": _s(4, I32), "lki": _s(32, I32), "spi": _s(1, I32), "wt": _s(512, BF), "kcs": _s(C, X4), "kss": _s(C, U8),
     "pidx": _s(1, I32), "pm": _s(6, I32), "pf": _s(6), "six": _s(1), "v32": _s(1), "vhf": _s(1), "vsum": _s(1), "ones": _s(32),
     "i_exp": _s(32, I32), "expk": _s(32, U16), "i_sel": _s(16), "sel": _s(16, U16), "i_e3": _s(12), "exp3": _s(12, U16),
-    "i_dup": _s(4), "dup": _s(4, U16), "i_il": _s(3), "il": _s(3, U16), "d2": _s(16), "d2p": _s(16), "i_d3": _s(24), "d3": _s(24),
+    "i_dup": _s(4), "dup": _s(4, U16), "i_il": _s(3), "il": _s(3, U16), "i_d3": _s(24), "d3": _s(24),
     "i_vj": _s(256), "cj": _s(256), "i_v3": _s(384), "v3": _s(384), "zt": _s(512, BF), "zc": _s(128, X4), "zs": _s(128, U8),
-    "lkf": _s(32), "at": _s(32), "spf": _s(1), "spx": _s(32), "spb": _s(32), "r1": _s(16), "r2": _s(16), "r3": _s(16), "r12": _s(16), "rr": _s(16),
+    "lkf": _s(32), "at": _s(32), "spf": _s(1), "spx": _s(32), "spb": _s(32), "r1": _s(16), "r2": _s(16), "r3": _s(16), "r12": _s(16), "r123": _s(16), "rr": _s(16),
     "xa": _s(512), "fa": _s(512), "fs": _s(256), "vk": _s(256),
-    "kb": _s(12, I32), "x1": _s(384), "b1": _s(384), "b1u": _s(384, U16), "cmp": _s(16 * 384, BF), "sc": _s(M1 * 192 + 1, BF), "js": _s(A1 * 384, BF),
-    "rc": _s(17), "qu": _s(24), "qo": _s(17), "fl": _s(16),
-    "q0": _s(16), "tot": _s(1), "ct": _s(64), "ctt": _s(64), "st": _s(64), "bt": _s(32), "qq": _s(16), "e1": _s(16), "e2": _s(16), "o1": _s(16), "o2": _s(16), "off": _s(16, U16),
+    "kb": _s(12, I32), "x1": _s(384), "b1": _s(384), "b1u": _s(256, U16), "cmp": _s(16 * 256, BF), "sc": _s(16 * 128 + 1, BF), "js": _s(16 * 128, BF),
+    "rc": _s(33), "qu": _s(33), "qo": _s(33, I32), "par": _s(16, I32), "fv": _s(16), "fl": _s(16),
+    "q0": _s(16), "tot": _s(1), "ct": _s(64), "ctt": _s(64), "st": _s(64), "bt": _s(32), "qq": _s(16), "e1": _s(16), "e2": _s(16), "o2": _s(16), "off": _s(16, U16),
     "wk": _s(NS + 256), "tk": _s(NS), "zi": _s(24, I32), "ki": _s(24, I32), "ji": _s(24, I32), "bz": _s(24), "ho": _s(24), "kz": _s(24), "zj": _s(32),
     "sw1": _s(32), "sw2": _s(64), "sw3": _s(64), "lj": _s(48, U16),
     "pc0": _s(CAPP, X4), "pc1": _s(CAPP, X4), "pc2": _s(CAPP, X4), "pc3": _s(CAPP, X4),
     "ps0": _s(CAPP, U8), "ps1": _s(CAPP, U8), "ps2": _s(CAPP, U8), "ps3": _s(CAPP, U8),
-    "ap": _s(24), "x3": _s(SL), "b3": _s(SL), "b3u": _s(SL, U16), "cmp3": _s(24 * SL, BF), "sc3": _s(M3 * SL // 2 + 1), "j3": _s(A3 * SL, BF), "rs3": _s(24),
-    "rc3": _s(24), "qu3": _s(24), "qo3": _s(24), "vm": _s(24), "vd1": _s(24), "vd": _s(24), "p1": _s(24), "p2": _s(24), "off3": _s(24, U16),
-    "wo": _s(S + 384), "to": _s(S), "zo": _s(32), "so1": _s(32), "so2": _s(64), "so3": _s(64), "lf": _s(48, U16),
+    "ap": _s(24), "x3": _s(SL), "b3": _s(SL), "b3u": _s(SL, U16), "cmp3": _s(M3 * SL, "float16"), "sc3": _s(M3 * SL // 2 + 1, "float16"), "j3": _s(A3 * SL, BF), "rs3": _s(24),
+    "rc3": _s(24), "qu3": _s(24), "qo3": _s(24), "vs": _s(24), "vd": _s(24), "p2": _s(24), "off3": _s(24, U16),
+    "wo": _s(NS + 384), "to": _s(S), "zo": _s(32), "so1": _s(32), "so2": _s(64), "so3": _s(64), "lf": _s(48, U16),
     "fw": _s(Z0 + NS, X4), "fsc": _s(Z0 + NS, U8), "oq": _s(S, X4), "os_": _s(S, U8), "wq": _s(128, X4), "wsc": _s(128, U8),
     "kf": _s(Z0 + NS), "okf": _s(S), "yw": _s(Z0 + NS), "ys": _s(S), "pz": ("psum", [128, 512 * N], "float32"),
 }
@@ -64,7 +66,7 @@ def rank_program(g, core, T, topo):
     def vop(deps, name, *a):
         need("v", deps)
         f = {"copy": vec.tensor_copy, "tt": vec.tensor_tensor, "ts": vec.tensor_scalar, "tr": vec.transpose, "scan": vec.tensor_tensor_scan,
-             "red": vec.tensor_reduce, "set": vec.memset, "q": vec.quantize_mx}[name]
+             "set": vec.memset, "q": vec.quantize_mx}[name]
         return done(f(*a), "v")
 
     def sop(deps, *a, **k):
@@ -112,7 +114,7 @@ def rank_program(g, core, T, topo):
     iota(T.i_e3[:], [[1, NB], [0, 2]], 0)
     iota(T.i_dup[:], [[16, 2], [0, 2]], 0)
     iota(T.i_il[:], [[8, 3]], 0)
-    t_ic = iota(T.i_d3[:], [[16, 24]], S)
+    t_ic = iota(T.i_d3[:], [[16, 24]], NS)
     low = [d for d in others if d < r]
     if low:
         need("g", [t_kl])
@@ -126,9 +128,9 @@ def rank_program(g, core, T, topo):
     t_wo = iota(T.wo[:, 0:S], [[0, S]], 0)
 
     vop([], "set", T.ones[:], 1.0)
-    for name in ("zj", "st", "zo"):
-        vop([], "set", T[name][:], 0.0)
-    vop([], "set", T.sc3[:, 0:1], 0.0)
+    vop([], "set", T.zj[:], 0.0)
+    vop([], "set", T.zo[:], 0.0)
+    vop([], "set", T.st[:], -1.0)
     vop([], "set", T.sc[:, 0:1], 0.0)
     t_zt = vop([], "set", T.zt[:], 0.0)
     need("v", [t_pi])
@@ -144,10 +146,9 @@ def rank_program(g, core, T, topo):
     t_sel = vop([], "ts", T.sel[:], T.i_sel[:], T.pf[:, 1:2], None, OP.add)
     vop([], "ts", T.dup[:], T.i_dup[:], T.pf[:, 0:1], None, OP.add)
     vop([], "ts", T.d3[:], T.i_d3[:], T.pf[:, 0:1], None, OP.add)
-    t_d2 = vop([], "ts", T.d2[:], T.i_d3[:, 0:16], T.pf[:, 0:1], float(NS - S), OP.add, OP.add)
+    vop([], "ts", T.sc3[:, 0:1], T.pf[:, 0:1], 0.0, R0, OP.mult, OP.add)
     t = vop([t], "ts", T.vsum[:], T.v32[:], T.vhf[:], None, OP.add)
     vop([], "ts", T.exp3[:], T.i_e3[:], T.six[:], None, OP.add)
-    vop([t_d2], "ts", T.d2p[:], T.d2[:], 1.0, None, OP.add)
     t_c = vop([t], "ts", T.il[:], T.i_il[:], T.vsum[:], None, OP.add)
     t_lkf = vop([t_lk], "copy", T.lkf[:], T.lki[:])
     t_at = vop([t_lkf], "tr", T.at[:], T.lkf[:])
@@ -158,8 +159,9 @@ def rank_program(g, core, T, topo):
     vop([t_spb], "ts", T.r1[:], T.at[:, 0:16], T.spb[:, 0:1], float(SL), OP.is_ge, OP.mult)
     t_r = vop([], "ts", T.r2[:], T.at[:, 0:16], T.spb[:, 1:2], float(SL), OP.is_ge, OP.mult)
     t_r3 = vop([], "ts", T.r3[:], T.at[:, 0:16], T.spb[:, 2:3], float(SL), OP.is_ge, OP.mult)
-    t_r12 = vop([t_r], "tt", T.r12[:], T.r1[:], T.r2[:], OP.add)
-    t_rr = vop([t_r12, t_r3], "tt", T.rr[:], T.r12[:], T.r3[:], OP.add)
+    t_r = vop([t_r], "tt", T.r12[:], T.r1[:], T.r2[:], OP.add)
+    t_r = vop([t_r, t_r3], "tt", T.r123[:], T.r12[:], T.r3[:], OP.add)
+    t_rr = vop([t_r], "ts", T.rr[:], T.r123[:], -1.0, None, OP.add)
     t_fa = vop([t_xa], "tr", T.fa[:], T.xa[:])
     t_fs = sop([t_fa, t_sel], T.fs[:], T.fa[:].indirect(T.sel[:]), AF.Copy)
     t_cj = vop([t_ivj], "ts", T.cj[:], T.i_vj[:], 65536.0, 1.0, OP.mult, OP.add)
@@ -178,36 +180,41 @@ def rank_program(g, core, T, topo):
         t_f = vop([], "set", T.fl[:], 1.0)
     else:
         W = 128 * nl
-        H = W // 2
+        WV, H = W - 128, W // 2
         total["kin"] = KE * nl
         t_kin = ("kin", KE * nl)
         t2 = sop([t_kin, t_ek], T.x1[:, H:W], T.kb[:, 0:4 * nl].indirect(T.expk[:, 4 * nl:8 * nl]), AF.Copy)
         t = vop([t_kin], "copy", T.x1[:, 0:H], T.kb[:, 0:4 * nl].indirect(T.expk[:, 0:4 * nl]))
-        t = vop([t, t2], "tr", T.b1[:, 0:W], T.x1[:, 0:W])
-        t = vop([t], "copy", T.b1u[:, 0:W], T.b1[:, 0:W])
+        t_b = vop([t, t2], "tr", T.b1[:, 0:W], T.x1[:, 0:W])
         for c in range(16):
-            t = vop([t] if c == 0 else [], "ts", T.cmp[:, W * c:W * (c + 1)], T.b1u[:, 0:W], T.at[:, c:c + 1], None, OP.is_equal)
-            if c < A1:
-                t_s = sop([t], T.js[:, W * c:W * (c + 1)], T.cmp[:, W * c:W * (c + 1)], AF.Copy, accum_out=T.rc[:, c:c + 1])
-        t = vop([t], "scan", T.sc[:, 1:M1 * H + 1], T.cmp[:, A1 * W:16 * W:2], T.cmp[:, A1 * W + 1:16 * W:2], 0.0, OP.add, OP.add)
-        t = vop([t], "copy", T.rc[:, A1:17], T.sc[:, 0:M1 * H + 1:H])
+            t_s = sop([t_b, t_at], T.js[:, 128 * c:128 * c + 128], T.b1[:, WV:W], AF.Sign, bias=T.at[:, c:c + 1], scale=-1.0, accum_out=T.rc[:, c:c + 1])
+        if nl > 1:
+            H = WV // 2
+            t = vop([t_b], "copy", T.b1u[:, 0:WV], T.b1[:, 0:WV])
+            for c in range(16):
+                t = vop([t] if c == 0 else [], "ts", T.cmp[:, WV * c:WV * (c + 1)], T.b1u[:, 0:WV], T.at[:, c:c + 1], None, OP.is_equal)
+            t = vop([t], "scan", T.sc[:, 1:16 * H + 1], T.cmp[:, 0:16 * WV:2], T.cmp[:, 1:16 * WV:2], 0.0, OP.add, OP.add)
+            t = vop([t], "copy", T.rc[:, 16:33], T.sc[:, 0:16 * H + 1:H])
         need("v", [t_s])
-        t = quads(t, T.rc, T.qu, T.qo, 17)
-        vop([t], "ts", T.fl[:, 0:A1], T.qo[:, 0:A1], 0.0, None, OP.is_equal)
-        t_f = vop([], "tt", T.fl[:, A1:16], T.qo[:, A1 + 1:17], T.qo[:, A1:16], OP.is_equal)
+        t = quads(t, T.rc, T.qu, T.qo, 33 if nl > 1 else 16)
+        t_p = vop([t], "ts", T.par[:], T.qo[:, 0:16], 1, None, OP.bitwise_and)
+        if nl > 1:
+            t = vop([], "tt", T.fv[:], T.qo[:, 17:33], T.qo[:, 16:32], OP.is_equal)
+            t_f = vop([t, t_p], "tt", T.fl[:], T.fv[:], T.par[:], OP.is_gt)
+        else:
+            t_f = vop([t_p], "ts", T.fl[:], T.par[:], 0.0, None, OP.is_equal)
 
     t_tot = sop([t_f], T.js[:, 0:16], T.fl[:], AF.Copy, accum_out=T.tot[:])
-    t_q = vop([t_f, t_rr], "scan", T.q0[:], T.rr[:], T.fl[:], 0.0, OP.max, OP.add)
-    t_e = vop([t_c], "tt", T.e1[:], T.d2p[:], T.fl[:], OP.mult)
+    t_q = vop([t_f, t_rr], "scan", T.q0[:], T.rr[:], T.fl[:], -1.0, OP.max, OP.add)
+    t_e = vop([t_c], "ts", T.e1[:], T.fl[:], 0.0, None, OP.is_equal)
     vop([t_q], "ts", T.ct[:, 0:32], T.ones[:], T.q0[:, 15:16], None, OP.mult)
     t = vop([t_tot], "ts", T.ct[:, 32:64], T.ones[:], T.tot[:], None, OP.mult)
-    t2 = vop([t_e], "tt", T.e2[:], T.d2[:], T.e1[:], OP.subtract)
+    t2 = vop([t_e], "tt", T.e2[:], T.d3[:, 0:16], T.e1[:], OP.mult)
     t = vop([t], "tr", T.ctt[:], T.ct[:])
-    t = vop([t], "scan", T.st[:, 1:33], T.ctt[:, 32:64], T.ctt[:, 0:32], 0.0, OP.add, OP.max)
+    t = vop([t], "scan", T.st[:, 1:33], T.ctt[:, 32:64], T.ctt[:, 0:32], -1.0, OP.add, OP.max)
     t = vop([t], "tr", T.bt[:], T.st[:, 0:32])
     t = vop([t], "scan", T.qq[:], T.rr[:], T.fl[:], T.bt[:, 0:1], OP.max, OP.add)
-    t = vop([t], "tt", T.o1[:], T.qq[:], T.fl[:], OP.mult)
-    t = vop([t, t2], "tt", T.o2[:], T.o1[:], T.e2[:], OP.add)
+    t = vop([t, t2], "tt", T.o2[:], T.qq[:], T.e2[:], OP.max)
     t_off = vop([t], "copy", T.off[:], T.o2[:])
 
     t = vop([t_off, t_vk, t_wk], "copy", T.wk[:].indirect(T.off[:]), T.vk[:])
@@ -258,23 +265,23 @@ def rank_program(g, core, T, topo):
     total["slk"] = KE * (N - 1)
     total["colc"] = total["cols"] = sum(len(eng[d]) for d in others)
     t_in = [("slk", total["slk"]), t_own]
-    t = vop(t_in, "copy", T.x3[:], T.ap[:].indirect(T.exp3[:]))
-    t_vm = vop([], "ts", T.vm[:], T.ap[:], 65536.0, None, OP.is_lt)
-    t_b3 = vop([t], "tr", T.b3[:], T.x3[:])
+    H = SL // 2
+    t2 = sop(t_in + [t_c], T.x3[:, H:SL], T.ap[:].indirect(T.exp3[:, NB:2 * NB]), AF.Copy)
+    t = vop(t_in, "copy", T.x3[:, 0:H], T.ap[:].indirect(T.exp3[:, 0:NB]))
+    t_b3 = vop([t, t2], "tr", T.b3[:], T.x3[:])
     for x in range(A3):
         t_s = sop(t_in + [t_b3], T.j3[:, SL * x:SL * (x + 1)], T.b3[:], AF.Sign, bias=T.ap[:, x:x + 1], scale=-1.0, accum_out=T.rs3[:, x:x + 1])
     t = vop([t_b3], "copy", T.b3u[:], T.b3[:])
-    H = SL // 2
     need("v", [t])
-    for x in range(A3, 24):
-        t = vop([], "ts", T.cmp3[:, SL * x:SL * (x + 1)], T.b3u[:], T.ap[:, x:x + 1], None, OP.is_lt)
-    t = vop([t], "scan", T.sc3[:, 1:M3 * H + 1], T.cmp3[:, A3 * SL:24 * SL:2], T.cmp3[:, A3 * SL + 1:24 * SL:2], 0.0, OP.add, OP.add)
-    t_vd = vop([t_vm], "tt", T.vd1[:], T.d3[:], T.vm[:], OP.mult)
+    for x in range(M3):
+        t = vop([], "ts", T.cmp3[:, SL * x:SL * (x + 1)], T.b3u[:], T.ap[:, A3 + x:A3 + x + 1], None, OP.is_lt)
+    t_vs = vop([], "ts", T.vs[:], T.ap[:], 65536.0, None, OP.is_ge)
+    t = vop([t], "scan", T.sc3[:, 1:M3 * H + 1], T.cmp3[:, 0:M3 * SL:2], T.cmp3[:, 1:M3 * SL:2], R0, OP.add, OP.add)
+    t_vd = vop([t_vs], "tt", T.vd[:], T.d3[:], T.vs[:], OP.mult)
     t = vop([t], "tt", T.rc3[:, A3:24], T.sc3[:, H:M3 * H + 1:H], T.sc3[:, 0:(M3 - 1) * H + 1:H], OP.subtract)
-    vop([t_vd], "tt", T.vd[:], T.d3[:], T.vd1[:], OP.subtract)
     if r == 0:
         own()
-    t = vop([t_s], "ts", T.rc3[:, 0:A3], T.rs3[:, 0:A3], 0.5, SL / 2 - 0.125, OP.mult, OP.add)
+    t = vop([t, t_s], "ts", T.rc3[:, 0:A3], T.rs3[:, 0:A3], 0.5, SL / 2 - 0.125, OP.mult, OP.add)
     t_v3 = sop([t_iv3, t_pf], T.v3[:], T.i_v3[:], AF.Identity, bias=T.pf[:, 2:3])
     for s in range(N):
         t_kc = sop([t_kf], T.kf[0:32, Z0 + SL * s:Z0 + SL * (s + 1)], T.b3[32 * s:32 * s + 32, :], AF.Copy)
@@ -284,8 +291,7 @@ def rank_program(g, core, T, topo):
         t_t = done(g.tensor.matmul_mx(T.pz[:, 512 * s:512 * s + CAPP], T.wq[:], T.wsc[:], T.fw[:, a:a + CAPP], T.fsc[:, a:a + CAPP], True, True), "t")
         t_y = sop([t_t, t_yw], T.yw[:, a:a + CAPP], T.pz[:, 512 * s:512 * s + CAPP], AF.Copy)
     t = quads(t, T.rc3, T.qu3, T.qo3, 24)
-    t = vop([t], "tt", T.p1[:], T.qo3[:], T.vm[:], OP.mult)
-    t = vop([t], "tt", T.p2[:], T.p1[:], T.vd[:], OP.add)
+    t = vop([t, t_vd], "tt", T.p2[:], T.qo3[:], T.vd[:], OP.max)
     t = vop([t], "copy", T.off3[:], T.p2[:])
     t = vop([t, t_v3, t_wo], "copy", T.wo[:].indirect(T.off3[:]), T.v3[:])
     t = vop([t], "tr", T.to[:], T.wo[:, 0:S])
@@ -299,11 +305,11 @@ def rank_program(g, core, T, topo):
         dma("y", [t], T.oc[:, 4 * lo:4 * hi], T.oq[:, lo:hi].bitcast(dt.uint8), "st1")
     for i in range(4):
         dma("y", [t_sc], T.osc[4 * i:4 * i + 4, :], T.os_[32 * i:32 * i + 4, :], "st1")
-    for c in range(S // CH):
-        lo, hi = c * CH, (c + 1) * CH
-        t = vop([t_y], "copy", T.ys[:, lo:hi], T.yw[:].indirect(T.lf[:, lo // 16:hi // 16]))
-        dma("y", [t], T.y[:, lo:hi], T.ys[:, lo:hi], "st1")
-    t = sop([t_kc, t_lf], T.okf[:], T.kf[:].indirect(T.lf[:, 0:S // 16]), AF.Copy)
-    dma("s", [t], T.ok[0:1, :], T.okf[0:1, :], "st2")
+    t = vop([t_y], "copy", T.ys[:, 0:YV], T.yw[:].indirect(T.lf[:, 0:YV // 16]))
+    dma("y", [t], T.y[:, 0:YV], T.ys[:, 0:YV], "st1")
+    t = sop([t_y, t_lf], T.ys[:, YV:S], T.yw[:].indirect(T.lf[:, YV // 16:S // 16]), AF.Copy)
+    t2 = sop([t_kc], T.okf[:], T.kf[:].indirect(T.lf[:, 0:S // 16]), AF.Copy)
+    dma("y", [t], T.y[:, YV:S], T.ys[:, YV:S], "st1")
+    dma("s", [t2], T.ok[0:1, :], T.okf[0:1, :], "st2")
     dma("s", [], T.ok[1:2, :], T.okf[32:33, :], "st2")
     need("g", list(total.items()))

from concourse.bass import DstId, RemoteDMATransfer
from concourse.mybir import dt, AluOpType as OP, ActivationFunctionType as AF

N, C, S, CAPP = 4, 512, 640, 176
SL = 192
NB = SL // 32
NS = N * SL
Z0 = 32
BIG = 70000.0
CH = 320
YV = 384
A3 = 11
M3 = 24 - A3
R0 = -float(M3 * SL // 2)


def _s(n, d="float32"):
    return ("sbuf", [128, n], d)


X4, U8, U16, BF, I32 = "float8_e4m3fn_x4", "uint8", "uint16", "bfloat16", "int32"
SCRATCH = {
    "kl": _s(4, I32), "lki": _s(32, I32), "spi": _s(1, I32), "wt": _s(512, BF), "kcs": _s(C, X4), "kss": _s(C, U8),
    "pidx": _s(1, I32), "pm": _s(6, I32), "pf": _s(6), "six": _s(1), "v32": _s(1), "vhf": _s(1), "vsum": _s(1), "ones": _s(32),
    "i_exp": _s(32, I32), "expk": _s(32, U16), "i_sel": _s(16), "sel": _s(16, U16), "i_e3": _s(12), "exp3": _s(12, U16),
    "i_dup": _s(4), "dup": _s(4, U16), "i_il": _s(3), "il": _s(3, U16), "i_d3": _s(24), "d3": _s(24),
    "i_vj": _s(256), "cj": _s(256), "i_v3": _s(384), "v3": _s(384), "zt": _s(512, BF), "zc": _s(128, X4), "zs": _s(128, U8),
    "lkf": _s(32), "at": _s(32), "spf": _s(1), "spx": _s(32), "spb": _s(32), "r1": _s(16), "r2": _s(16), "r3": _s(16), "r12": _s(16), "r123": _s(16), "rr": _s(16),
    "xa": _s(512), "fa": _s(512), "fs": _s(256), "vk": _s(256),
    "kb": _s(12, I32), "x1": _s(384), "b1": _s(384), "b1u": _s(256, U16), "cmp": _s(16 * 256, BF), "sc": _s(16 * 128 + 1, BF), "js": _s(16 * 128, BF),
    "rc": _s(33), "qu": _s(33), "qo": _s(33, I32), "par": _s(16, I32), "fv": _s(16), "fl": _s(16),
    "q0": _s(16), "tot": _s(1), "ct": _s(64), "ctt": _s(64), "st": _s(64), "bt": _s(32), "qq": _s(16), "e1": _s(16), "e2": _s(16), "o2": _s(16), "off": _s(16, U16),
    "wk": _s(NS + 256), "tk": _s(NS), "zi": _s(24, I32), "ki": _s(24, I32), "ji": _s(24, I32), "bz": _s(24), "ho": _s(24), "kz": _s(24), "zj": _s(32),
    "sw1": _s(32), "sw2": _s(64), "sw3": _s(64), "lj": _s(48, U16),
    "pc0": _s(CAPP, X4), "pc1": _s(CAPP, X4), "pc2": _s(CAPP, X4), "pc3": _s(CAPP, X4),
    "ps0": _s(CAPP, U8), "ps1": _s(CAPP, U8), "ps2": _s(CAPP, U8), "ps3": _s(CAPP, U8),
    "ap": _s(24), "x3": _s(SL), "b3": _s(SL), "b3u": _s(SL, U16), "cmp3": _s(M3 * SL, "float16"), "sc3": _s(M3 * SL // 2 + 1, "float16"), "j3": _s(A3 * SL, BF), "rs3": _s(24),
    "rc3": _s(24), "qu3": _s(24), "qo3": _s(24), "vs": _s(24), "vd": _s(24), "p2": _s(24), "off3": _s(24, U16),
    "wo": _s(NS + 384), "to": _s(S), "zo": _s(32), "so1": _s(32), "so2": _s(64), "so3": _s(64), "lf": _s(48, U16),
    "fw": _s(Z0 + NS, X4), "fsc": _s(Z0 + NS, U8), "oq": _s(S, X4), "os_": _s(S, U8), "wq": _s(128, X4), "wsc": _s(128, U8),
    "kf": _s(Z0 + NS), "okf": _s(S), "yw": _s(Z0 + NS), "ys": _s(S), "pz": ("psum", [128, 512 * N], "float32"),
}
SEMAPHORES = ["v", "s", "t", "gi", "dkl", "dlk", "dsp", "dw", "dk", "dz", "kin", "slk", "colc", "cols", "lsent", "own", "st1", "st2"]


def rank_program(g, core, T, topo):
    r = T.rank_of(core)
    if r is None:
        return
    Q = {"v": g.vector, "s": g.scalar, "t": g.tensor, "g": g, "y": g.sync}
    seen, total = {}, {}

    def need(q, toks):
        for tok in toks:
            if tok is not None and seen.get((q, tok[0]), 0) < tok[1]:
                Q[q].wait_ge(T.sem[tok[0]], tok[1])
                seen[(q, tok[0])] = tok[1]

    def done(inst, sem, n=1):
        inst.then_inc(T.sem[sem], n)
        total[sem] = total.get(sem, 0) + n
        return (sem, total[sem])

    vec, act = g.vector, g.scalar

    def vop(deps, name, *a):
        need("v", deps)
        f = {"copy": vec.tensor_copy, "tt": vec.tensor_tensor, "ts": vec.tensor_scalar, "tr": vec.transpose, "scan": vec.tensor_tensor_scan,
             "set": vec.memset, "q": vec.quantize_mx}[name]
        return done(f(*a), "v")

    def sop(deps, *a, **k):
        need("s", deps)
        return done(act.activation(*a, **k), "s")

    def dma(q, deps, out, in_, sem):
        need(q, deps)
        return done(Q[q].dma_start(out, in_), sem, 16)

    others = [d for d in range(N) if d != r]
    far = [d for d in others if topo.chip(T.cores[d]) != topo.chip(core)]
    near = [d for d in others if d not in far]
    fe = topo.engines(core, T.cores[far[0]])
    KE = len(fe) // len(far)
    eng = {d: fe[i * KE:(i + 1) * KE] for i, d in enumerate(far)}
    for d in near:
        eng[d] = [e for e in topo.engines(core, T.cores[d]) if e not in fe]

    def send(dests, sem, src, dst, few):
        tr = []
        for d in dests:
            rid, pid, _ = topo.addr(T.cores[d])
            m = sum(1 << e for e in (eng[d][:KE] if few else eng[d]))
            tr.append(RemoteDMATransfer(dst_ids=[DstId(rid=rid, pnc=pid)], dma_engine_mask=m, remote_sem=T.sem[sem], src=src(d), dst=dst(d)))
            total["lsent"] = total.get("lsent", 0) + (KE if few else len(eng[d]))
        g.remote_dma_fused(tr, local_sem=T.sem.lsent)

    t_kl = dma("y", [], T.kl[:], T.ky[:], "dkl")
    for a in range(8):
        t_lk = dma("ys"[a % 2], [], T.lki[16 * a:16 * a + 16, :], T.ky[:], "dlk")
    for a in range(8):
        t_sp = dma("ys"[a % 2], [], T.spi[16 * a:16 * a + 16, :], T.sp[:], "dsp")
    dma("y", [], T.kcs[:].bitcast(dt.uint8), T.kc[:], "dk")
    t_k = dma("y", [], T.kss[:], T.ks[:], "dk")
    t_w = dma("y", [], T.wt[:], T.w[:], "dw")

    def iota(out, pat, base, cm=0, i32=False):
        if i32:
            return done(g.iota(out, pat, base, cm), "gi")
        return done(g.iota(out, pat, base, cm, allow_small_or_imprecise_dtypes=True), "gi")
    t_pi = iota(T.pidx[:], [[0, 1]], 0, 1, True)
    t_ie = iota(T.i_exp[:], [[1, 16], [0, 2]], 0, 0, True)
    iota(T.i_sel[:], [[32, 16]], 0)
    iota(T.i_e3[:], [[1, NB], [0, 2]], 0)
    iota(T.i_dup[:], [[16, 2], [0, 2]], 0)
    iota(T.i_il[:], [[8, 3]], 0)
    t_ic = iota(T.i_d3[:], [[16, 24]], NS)
    low = [d for d in others if d < r]
    if low:
        need("g", [t_kl])
        send(low, "kin", lambda d: T.kl[:], lambda d: T.kb[:, 4 * (r - d - 1):4 * (r - d)], True)
    t_ivj = iota(T.i_vj[:], [[1, 16], [16, 16]], 0)
    t_wk = iota(T.wk[:, 0:NS], [[0, NS]], -1)
    t_iv3 = iota(T.i_v3[:], [[32, 24], [1, 16]], Z0)
    iota(T.kf[:, 0:Z0], [[0, Z0]], -1)
    t_kf = iota(T.kf[:, Z0:Z0 + NS], [[1, N], [0, SL]], 0)
    t_yw = iota(T.yw[:], [[0, Z0 + NS]], 0)
    t_wo = iota(T.wo[:, 0:S], [[0, S]], 0)

    vop([], "set", T.ones[:], 1.0)
    vop([], "set", T.zj[:], 0.0)
    vop([], "set", T.zo[:], 0.0)
    vop([], "set", T.st[:], -1.0)
    vop([], "set", T.sc[:, 0:1], 0.0)
    t_zt = vop([], "set", T.zt[:], 0.0)
    need("v", [t_pi])
    for i, b in enumerate((15, 31, 16, 1, 14)):
        vop([], "ts", T.pm[:, i:i + 1], T.pidx[:], b, None, OP.bitwise_and)
    t = vop([], "ts", T.pm[:, 5:6], T.pidx[:], 5, None, OP.arith_shift_right)
    t_pf = vop([t], "copy", T.pf[:], T.pm[:])
    t_ek = vop([t_ie], "copy", T.expk[:], T.i_exp[:])
    need("v", [t_pf, t_ic])
    vop([], "ts", T.six[:], T.pf[:, 5:6], float(NB), None, OP.mult)
    vop([], "ts", T.v32[:], T.pf[:, 3:4], 32.0, None, OP.mult)
    t = vop([], "ts", T.vhf[:], T.pf[:, 4:5], 0.5, None, OP.mult)
    t_sel = vop([], "ts", T.sel[:], T.i_sel[:], T.pf[:, 1:2], None, OP.add)
    vop([], "ts", T.dup[:], T.i_dup[:], T.pf[:, 0:1], None, OP.add)
    vop([], "ts", T.d3[:], T.i_d3[:], T.pf[:, 0:1], None, OP.add)
    vop([], "ts", T.sc3[:, 0:1], T.pf[:, 0:1], 0.0, R0, OP.mult, OP.add)
    t = vop([t], "ts", T.vsum[:], T.v32[:], T.vhf[:], None, OP.add)
    vop([], "ts", T.exp3[:], T.i_e3[:], T.six[:], None, OP.add)
    t_c = vop([t], "ts", T.il[:], T.i_il[:], T.vsum[:], None, OP.add)
    t_lkf = vop([t_lk], "copy", T.lkf[:], T.lki[:])
    t_at = vop([t_lkf], "tr", T.at[:], T.lkf[:])
    t_xa = sop([t_at, t_ek], T.xa[:], T.at[:, 0:16].indirect(T.expk[:]), AF.Copy)
    t_spf = vop([t_sp], "copy", T.spf[:], T.spi[:])
    t_spx = vop([t_spf], "ts", T.spx[:], T.ones[:], T.spf[:], None, OP.mult)
    t_spb = vop([t_spx], "tr", T.spb[:], T.spx[:])
    vop([t_spb], "ts", T.r1[:], T.at[:, 0:16], T.spb[:, 0:1], float(SL), OP.is_ge, OP.mult)
    t_r = vop([], "ts", T.r2[:], T.at[:, 0:16], T.spb[:, 1:2], float(SL), OP.is_ge, OP.mult)
    t_r3 = vop([], "ts", T.r3[:], T.at[:, 0:16], T.spb[:, 2:3], float(SL), OP.is_ge, OP.mult)
    t_r = vop([t_r], "tt", T.r12[:], T.r1[:], T.r2[:], OP.add)
    t_r = vop([t_r, t_r3], "tt", T.r123[:], T.r12[:], T.r3[:], OP.add)
    t_rr = vop([t_r], "ts", T.rr[:], T.r123[:], -1.0, None, OP.add)
    t_fa = vop([t_xa], "tr", T.fa[:], T.xa[:])
    t_fs = sop([t_fa, t_sel], T.fs[:], T.fa[:].indirect(T.sel[:]), AF.Copy)
    t_cj = vop([t_ivj], "ts", T.cj[:], T.i_vj[:], 65536.0, 1.0, OP.mult, OP.add)
    t_vk = vop([t_cj, t_fs], "tt", T.vk[:], T.fs[:], T.cj[:], OP.add)

    nl = N - 1 - r

    def quads(tok, src, qu, qo, n):
        t = vop([tok], "tt", qu[0:64, 0:n], src[0:64, 0:n], src[64:128, 0:n], OP.add)
        need("v", [t])
        for b in range(4):
            t = vop([], "tt", qo[32 * b:32 * b + 32, 0:n], qu[0:32, 0:n], qu[32:64, 0:n], OP.add)
        return t

    if nl == 0:
        t_f = vop([], "set", T.fl[:], 1.0)
    else:
        W = 128 * nl
        WV, H = W - 128, W // 2
        total["kin"] = KE * nl
        t_kin = ("kin", KE * nl)
        t2 = sop([t_kin, t_ek], T.x1[:, H:W], T.kb[:, 0:4 * nl].indirect(T.expk[:, 4 * nl:8 * nl]), AF.Copy)
        t = vop([t_kin], "copy", T.x1[:, 0:H], T.kb[:, 0:4 * nl].indirect(T.expk[:, 0:4 * nl]))
        t_b = vop([t, t2], "tr", T.b1[:, 0:W], T.x1[:, 0:W])
        for c in range(16):
            t_s = sop([t_b, t_at], T.js[:, 128 * c:128 * c + 128], T.b1[:, WV:W], AF.Sign, bias=T.at[:, c:c + 1], scale=-1.0, accum_out=T.rc[:, c:c + 1])
        if nl > 1:
            H = WV // 2
            t = vop([t_b], "copy", T.b1u[:, 0:WV], T.b1[:, 0:WV])
            for c in range(16):
                t = vop([t] if c == 0 else [], "ts", T.cmp[:, WV * c:WV * (c + 1)], T.b1u[:, 0:WV], T.at[:, c:c + 1], None, OP.is_equal)
            t = vop([t], "scan", T.sc[:, 1:16 * H + 1], T.cmp[:, 0:16 * WV:2], T.cmp[:, 1:16 * WV:2], 0.0, OP.add, OP.add)
            t = vop([t], "copy", T.rc[:, 16:33], T.sc[:, 0:16 * H + 1:H])
        need("v", [t_s])
        t = quads(t, T.rc, T.qu, T.qo, 33 if nl > 1 else 16)
        t_p = vop([t], "ts", T.par[:], T.qo[:, 0:16], 1, None, OP.bitwise_and)
        if nl > 1:
            t = vop([], "tt", T.fv[:], T.qo[:, 17:33], T.qo[:, 16:32], OP.is_equal)
            t_f = vop([t, t_p], "tt", T.fl[:], T.fv[:], T.par[:], OP.is_gt)
        else:
            t_f = vop([t_p], "ts", T.fl[:], T.par[:], 0.0, None, OP.is_equal)

    t_tot = sop([t_f], T.js[:, 0:16], T.fl[:], AF.Copy, accum_out=T.tot[:])
    t_q = vop([t_f, t_rr], "scan", T.q0[:], T.rr[:], T.fl[:], -1.0, OP.max, OP.add)
    t_e = vop([t_c], "ts", T.e1[:], T.fl[:], 0.0, None, OP.is_equal)
    vop([t_q], "ts", T.ct[:, 0:32], T.ones[:], T.q0[:, 15:16], None, OP.mult)
    t = vop([t_tot], "ts", T.ct[:, 32:64], T.ones[:], T.tot[:], None, OP.mult)
    t2 = vop([t_e], "tt", T.e2[:], T.d3[:, 0:16], T.e1[:], OP.mult)
    t = vop([t], "tr", T.ctt[:], T.ct[:])
    t = vop([t], "scan", T.st[:, 1:33], T.ctt[:, 32:64], T.ctt[:, 0:32], -1.0, OP.add, OP.max)
    t = vop([t], "tr", T.bt[:], T.st[:, 0:32])
    t = vop([t], "scan", T.qq[:], T.rr[:], T.fl[:], T.bt[:, 0:1], OP.max, OP.add)
    t = vop([t, t2], "tt", T.o2[:], T.qq[:], T.e2[:], OP.max)
    t_off = vop([t], "copy", T.off[:], T.o2[:])

    t = vop([t_off, t_vk, t_wk], "copy", T.wk[:].indirect(T.off[:]), T.vk[:])
    t = vop([t], "tr", T.tk[:], T.wk[:, 0:NS])
    te, to = T.tk[:, 0:NS:32], T.tk[:, 16:NS:32]
    t_zi = vop([t], "tt", T.zi[:], te, to, OP.add)
    vop([t_zi], "ts", T.ki[:], T.zi[:], 65535, None, OP.bitwise_and)
    t = vop([], "ts", T.bz[:], T.zi[:], 0.0, BIG, OP.is_lt, OP.mult)
    t_kz = vop([t], "tt", T.kz[:], T.ki[:], T.bz[:], OP.add)
    need("g", [t_kz])
    send(others, "slk", lambda d: T.kz[:, NB * d:NB * (d + 1)], lambda d: T.ap[:, NB * r:NB * (r + 1)], True)
    t_own = dma("y", [t_kz], T.ap[:, NB * r:NB * (r + 1)], T.kz[:, NB * r:NB * (r + 1)], "own")

    def lists(tok, z, s1, s2, s3, out):
        t = vop([tok], "tr", s1[:], z[:])
        t = vop([t], "copy", s2[:], s1[:].indirect(T.dup[:]))
        t = vop([t], "tr", s3[:], s2[:])
        return vop([t], "copy", out[:], s3[:].indirect(T.il[:]))

    vop([], "ts", T.ji[:], T.zi[:], 16, None, OP.arith_shift_right)
    t = vop([], "ts", T.ho[:], to, 0.0, 256.0, OP.is_ge, OP.mult)
    t = vop([t], "tt", T.zj[:, 0:24], T.ji[:], T.ho[:], OP.add)
    t_lj = lists(t, T.zj, T.sw1, T.sw2, T.sw3, T.lj)

    def pick(d, oc, osc):
        L = T.lj[:, 12 * d:12 * d + CAPP // 16]
        return (vop([t_lj, t_k], "copy", oc.bitcast(dt.uint32), T.kcs[:].bitcast(dt.uint32).indirect(L)),
                sop([t_lj, t_k], osc, T.kss[:].indirect(L), AF.Copy))
    for d in far + near:
        t_pv, t_ps = pick(d, T["pc%d" % d][:], T["ps%d" % d][:])
    w0 = Z0 + SL * r
    need("g", [t_pv])
    send(far + near, "colc", lambda d: T["pc%d" % d][:].bitcast(dt.uint8), lambda d: T.fw[:, w0:w0 + CAPP].bitcast(dt.uint8), False)
    need("g", [t_ps])
    send(far + near, "cols", lambda d: T["ps%d" % d][:], lambda d: T.fsc[:, w0:w0 + CAPP], False)

    tk = {}

    def own():
        tk["v"], tk["s"] = pick(r, T.fw[:, w0:w0 + CAPP], T.fsc[:, w0:w0 + CAPP])
        t = vop([t_zt], "q", T.zc[:], T.zs[:], T.zt[:])
        dma("y", [t], T.fw[:, 0:Z0].bitcast(dt.uint8), T.zc[:, 0:Z0].bitcast(dt.uint8), "dz")
        tk["z"] = dma("y", [t], T.fsc[:, 0:Z0], T.zs[:, 0:Z0], "dz")
        tk["w"] = vop([t_w], "q", T.wq[:], T.wsc[:], T.wt[:])
    if r:
        own()

    total["slk"] = KE * (N - 1)
    total["colc"] = total["cols"] = sum(len(eng[d]) for d in others)
    t_in = [("slk", total["slk"]), t_own]
    H = SL // 2
    t2 = sop(t_in + [t_c], T.x3[:, H:SL], T.ap[:].indirect(T.exp3[:, NB:2 * NB]), AF.Copy)
    t = vop(t_in, "copy", T.x3[:, 0:H], T.ap[:].indirect(T.exp3[:, 0:NB]))
    t_b3 = vop([t, t2], "tr", T.b3[:], T.x3[:])
    for x in range(A3):
        t_s = sop(t_in + [t_b3], T.j3[:, SL * x:SL * (x + 1)], T.b3[:], AF.Sign, bias=T.ap[:, x:x + 1], scale=-1.0, accum_out=T.rs3[:, x:x + 1])
    t = vop([t_b3], "copy", T.b3u[:], T.b3[:])
    need("v", [t])
    for x in range(M3):
        t = vop([], "ts", T.cmp3[:, SL * x:SL * (x + 1)], T.b3u[:], T.ap[:, A3 + x:A3 + x + 1], None, OP.is_lt)
    t_vs = vop([], "ts", T.vs[:], T.ap[:], 65536.0, None, OP.is_ge)
    t = vop([t], "scan", T.sc3[:, 1:M3 * H + 1], T.cmp3[:, 0:M3 * SL:2], T.cmp3[:, 1:M3 * SL:2], R0, OP.add, OP.add)
    t_vd = vop([t_vs], "tt", T.vd[:], T.d3[:], T.vs[:], OP.mult)
    t = vop([t], "tt", T.rc3[:, A3:24], T.sc3[:, H:M3 * H + 1:H], T.sc3[:, 0:(M3 - 1) * H + 1:H], OP.subtract)
    if r == 0:
        own()
    t = vop([t, t_s], "ts", T.rc3[:, 0:A3], T.rs3[:, 0:A3], 0.5, SL / 2 - 0.125, OP.mult, OP.add)
    t_v3 = sop([t_iv3, t_pf], T.v3[:], T.i_v3[:], AF.Identity, bias=T.pf[:, 2:3])
    for s in range(N):
        t_kc = sop([t_kf], T.kf[0:32, Z0 + SL * s:Z0 + SL * (s + 1)], T.b3[32 * s:32 * s + 32, :], AF.Copy)
    for s in [r] + others:
        a = Z0 + SL * s
        need("t", [tk["w"]] + ([tk["v"], tk["s"]] if s == r else [("colc", total["colc"]), ("cols", total["cols"])]))
        t_t = done(g.tensor.matmul_mx(T.pz[:, 512 * s:512 * s + CAPP], T.wq[:], T.wsc[:], T.fw[:, a:a + CAPP], T.fsc[:, a:a + CAPP], True, True), "t")
        t_y = sop([t_t, t_yw], T.yw[:, a:a + CAPP], T.pz[:, 512 * s:512 * s + CAPP], AF.Copy)
    t = quads(t, T.rc3, T.qu3, T.qo3, 24)
    t = vop([t, t_vd], "tt", T.p2[:], T.qo3[:], T.vd[:], OP.max)
    t = vop([t], "copy", T.off3[:], T.p2[:])
    t = vop([t, t_v3, t_wo], "copy", T.wo[:].indirect(T.off3[:]), T.v3[:])
    t = vop([t], "tr", T.to[:], T.wo[:, 0:S])
    t = vop([t], "tt", T.zo[:, 0:20], T.to[:, 0:S:32], T.to[:, 16:S:32], OP.add)
    t_lf = lists(t, T.zo, T.so1, T.so2, T.so3, T.lf)

    t_sc = sop([t_lf, ("cols", total["cols"]), tk["s"], tk["z"]], T.os_[:], T.fsc[:].indirect(T.lf[:, 0:S // 16]), AF.Copy)
    for c in range(S // CH):
        lo, hi = c * CH, (c + 1) * CH
        t = vop([t_lf, ("colc", total["colc"]), tk["v"], tk["z"]], "copy", T.oq[:, lo:hi].bitcast(dt.uint32), T.fw[:].bitcast(dt.uint32).indirect(T.lf[:, lo // 16:hi // 16]))
        dma("y", [t], T.oc[:, 4 * lo:4 * hi], T.oq[:, lo:hi].bitcast(dt.uint8), "st1")
    for i in range(4):
        dma("y", [t_sc], T.osc[4 * i:4 * i + 4, :], T.os_[32 * i:32 * i + 4, :], "st1")
    t = vop([t_y], "copy", T.ys[:, 0:YV], T.yw[:].indirect(T.lf[:, 0:YV // 16]))
    dma("y", [t], T.y[:, 0:YV], T.ys[:, 0:YV], "st1")
    t = sop([t_y, t_lf], T.ys[:, YV:S], T.yw[:].indirect(T.lf[:, YV // 16:S // 16]), AF.Copy)
    t2 = sop([t_kc], T.okf[:], T.kf[:].indirect(T.lf[:, 0:S // 16]), AF.Copy)
    dma("y", [t], T.y[:, YV:S], T.ys[:, YV:S], "st1")
    dma("s", [t2], T.ok[0:1, :], T.okf[0:1, :], "st2")
    dma("s", [], T.ok[1:2, :], T.okf[32:33, :], "st2")
    need("g", list(total.items()))
